import numpy as np
import ml_dtypes


def mxq(x, axis, fmt="e4m3"):
    dtype, down = {"e4m3": (ml_dtypes.float8_e4m3fn, 7), "e5m2": (ml_dtypes.float8_e5m2, 14)}[fmt]
    v = np.moveaxis(np.asarray(x, np.float32).astype(ml_dtypes.bfloat16).astype(np.float64), axis, -1)
    blocks = v.reshape(v.shape[:-1] + (-1, 32))
    amax = np.abs(blocks).max(-1, keepdims=True)
    byte = np.maximum(np.where(amax > 0, np.frexp(amax)[1] - 1 + 127, 0) - down, 1)
    scale = np.exp2(byte - 127.0)
    codes = (blocks / scale).astype(np.float32).astype(dtype).astype(np.float64)
    return np.moveaxis((codes * scale).reshape(v.shape), -1, axis)


WIDE = False


def mx_kscale(k):
    if not WIDE:
        return np.ones(k)
    levels = np.array([10, -10, 5, -5, 0])
    if k % 512:
        return np.exp2(np.random.permutation(np.resize(levels, k // 32))).repeat(32)
    a = np.empty((k // 512, 16))
    for p in range(k // 512):
        a[p, :8] = np.random.permutation(np.resize(levels, 8))
        for g in range(8):
            far = levels[np.abs(levels - a[p, g]) >= 10]
            a[p, g + 8] = far[np.random.randint(len(far))]
    return np.exp2(a.ravel()).repeat(32)


BF16 = ml_dtypes.bfloat16


def bf(x):
    return np.asarray(x, np.float32).astype(BF16)


def f64(x):
    return np.asarray(x).astype(np.float64)


E2M1 = np.array([0.0, 0.5, 1.0, 1.5, 2.0, 3.0, 4.0, 6.0, -0.0, -0.5, -1.0, -1.5, -2.0, -3.0, -4.0, -6.0])


def pack_weight(w, fmt):
    k, n = w.shape
    w = f64(bf(w)).reshape(k // 32, 32, n)
    amax = np.abs(w).max(1)
    if fmt == "e4m3":
        byte = np.frexp(amax)[1] - 1 + 127 - 7
    else:
        mant, ex = np.frexp(amax / 6.0)
        byte = np.where(mant > 0.5, ex, ex - 1) + 127
    byte = np.clip(np.where(amax > 0, byte, 1), 1, 254)
    scaled = (w * np.exp2(127.0 - byte)[:, None, :]).reshape(k, n).astype(np.float32)
    by_word = np.ascontiguousarray(scaled.reshape(k // 512, 128, 4, n).transpose(0, 1, 3, 2))
    if fmt == "e4m3":
        words = by_word.astype(ml_dtypes.float8_e4m3fn).view(np.uint8)
    else:
        c = by_word.astype(ml_dtypes.float4_e2m1fn).view(np.uint8) & 0xF
        words = c[..., 0::2] | (c[..., 1::2] << 4)
    return np.ascontiguousarray(words), np.ascontiguousarray(byte.astype(np.uint8).reshape(k // 512, 16, n))


def unpack_weight(words, scales, fmt):
    g, p, n, _ = words.shape
    if fmt == "e4m3":
        vals = np.ascontiguousarray(words).view(ml_dtypes.float8_e4m3fn).astype(np.float64)
    else:
        nib = np.empty((g, p, n, 4), np.uint8)
        nib[..., 0::2] = words & 0xF
        nib[..., 1::2] = words >> 4
        vals = E2M1[nib]
    vals = vals * np.repeat(np.exp2(scales.astype(np.float64) - 127.0), 8, axis=1)[..., None]
    return vals.transpose(0, 1, 3, 2).reshape(g * 512, n)
def pack4(w):
    words, scales = pack_weight(w, "e2m1")
    return words.reshape(words.shape[0], 128, -1), scales


def unpack4(words, scales):
    return unpack_weight(words.reshape(words.shape[0], 128, -1, 2), scales, "e2m1")


def planes(Y):
    n, m = Y.shape
    b = f64(bf(Y)).reshape(n // 32, 32, m)
    amax = np.abs(b).max(1)
    byte = np.clip(np.where(amax > 0, np.frexp(amax)[1] - 1 + 127 - 7, 1), 1, 254)
    codes = (b * np.exp2(127.0 - byte)[:, None, :]).reshape(n, m).astype(np.float32).astype(ml_dtypes.float8_e4m3fn).view(np.uint8)
    words = codes.reshape(n // 512, 128, 4, m).transpose(0, 1, 3, 2)
    return np.ascontiguousarray(words), np.ascontiguousarray(byte.astype(np.uint8).reshape(n // 512, 16, m))


B, T, E, D = 2, 512, 1024, 1024


def sigmoid(v):
    return 1.0 / (1.0 + np.exp(-v))


def diagonal_masked_map(q, k):
    logits = (mxq(q, 2, "e4m3") @ mxq(k, 2, "e4m3").transpose(0, 2, 1)) / np.sqrt(E)
    pos = np.arange(T)
    on_diag = pos[:, None] == pos[None, :]
    logits = np.where(on_diag[None, :, :], -1e9, logits)
    e = np.exp(logits - logits.max(-1, keepdims=True))
    return e / e.sum(-1, keepdims=True)


def setup_inputs():
    s, t = mx_kscale(E), mx_kscale(T)
    qn = np.random.standard_normal((B, T, E))
    kn = np.random.standard_normal((B, T, E)) + 2.0 / np.sqrt(E) * qn
    g = bf((1.0 + 0.1 * np.random.standard_normal(T)) * t)
    wa_words, wa_scales = pack4(np.random.standard_normal((T, D)) / np.sqrt(T) / t[:, None])
    return {
        "q": bf(qn * s),
        "k": bf(kn / s),
        "g": g,
        "wa_words": wa_words,
        "wa_scales": wa_scales,
        "mb": bf(0.5 * np.random.standard_normal((B, T, D))),
        "x1": bf(np.random.standard_normal((B, T, D))),
        "x2": bf(np.random.standard_normal((B, T, D))),
    }


def core(q, k, g, wa_words, wa_scales, mb, x1, x2):
    a = diagonal_masked_map(f64(q), f64(k))
    c = f64(g)[None, None, :] * (T * a - 1.0)
    n = mxq(c, 2, "e4m3") @ unpack4(wa_words, wa_scales)
    eta = sigmoid(n + f64(mb))
    return (1.0 - eta) * f64(x1) + eta * f64(x2)


def reference(q, k, g, wa_words, wa_scales, mb, x1, x2):
    R_out = core(q, k, g, wa_words, wa_scales, mb, x1, x2)
    words, scales = planes(np.moveaxis(R_out, 1, 0).reshape(512, -1))
    return R_out, words, scales

@@ -1,0 +1,493 @@
+from contextlib import ExitStack
+
+import concourse.mybir as mybir
+from concourse.masks import make_identity
+
+B, T, E, D = 2, 512, 1024, 1024
+P = 128
+FLOPS = 2 * B * T * T * E + 2 * B * T * T * D
+
+F32 = mybir.dt.float32
+BF16 = mybir.dt.bfloat16
+U32 = mybir.dt.uint32
+I32 = mybir.dt.int32
+U8 = mybir.dt.uint8
+E4M3 = mybir.dt.float8_e4m3fn_x4
+E2M1 = mybir.dt.float4_e2m1fn_x4
+ALU = mybir.AluOpType
+ACT = mybir.ActivationFunctionType
+AX = mybir.AxisListType
+
+MASK = 2.0**20
+DSB = 3
+
+
+def tile_saitsdiagonalmaskedmapblend_x2_kernel(
+    tc, q, k, g, wa_words, wa_scales, mb, x1, x2, out_0, out_1, out_2
+):
+    nc = tc.nc
+    with ExitStack() as ctx:
+        keep = ctx.enter_context(tc.tile_pool(name="keep", bufs=1))
+        work = ctx.enter_context(tc.tile_pool(name="work", bufs=3))
+        psum = ctx.enter_context(tc.psum_pool(name="psum", bufs=2))
+
+        wa_s = keep.tile([P, D], U8, name="wa_s", align_bytes=64)
+        nc.vector.memset(wa_s[:].bitcast(I32), 0)
+        ident = keep.tile([P, P], F32, name="ident")
+        make_identity(nc, ident[:])
+        g_in = keep.tile([P, 4], BF16, name="g_in")
+        g512 = keep.tile([P, 4], F32, name="g512")
+
+        mask_codes, mask_scales, diags = [], [], []
+        for i, value in enumerate((MASK, -MASK)):
+            diag = keep.tile([P, 4 * P], BF16, name="diag%d" % i, align_bytes=64)
+            nc.gpsimd.memset(diag[:], 0.0)
+            nc.gpsimd.affine_select(
+                out=diag[:],
+                in_=diag[:],
+                compare_op=ALU.not_equal,
+                fill=value,
+                base=0,
+                pattern=[[-1, 4 * P]],
+                channel_multiplier=4,
+            )
+            diags.append(diag)
+            mask_codes.append(keep.tile([P, P], U32, name="mc%d" % i, align_bytes=64))
+            mask_scales.append(keep.tile([P, P], U8, name="ms%d" % i, align_bytes=64))
+        half = []
+        for i, value in enumerate((1.0, -1.0)):
+            hi = keep.tile([P, P], BF16, name="half%d" % i)
+            nc.gpsimd.tensor_scalar(out=hi[:], in0=ident[:], scalar1=value, scalar2=0.0, op0=ALU.mult, op1=ALU.add)
+            half.append(hi)
+
+        nc.scalar.dma_start(out=g_in[:], in_=g.rearrange("(p t) -> p t", t=4))
+        for quad in range(4):
+            nc.scalar.dma_start(
+                out=wa_s[32 * quad : 32 * quad + 4, :].bitcast(I32),
+                in_=wa_scales[0, 4 * quad : 4 * quad + 4, :].bitcast(I32),
+            )
+
+        def constants_g():
+            nc.vector.tensor_scalar_mul(g512[:], g_in[:], 512.0)
+
+        def constants_v():
+            for i in range(2):
+                nc.vector.quantize_mx(out=mask_codes[i][:].bitcast(E4M3), scales=mask_scales[i][:], in_=diags[i][:])
+
+        k_in, q_in, mb_in, x1_in, x2_in = {}, {}, {}, {}, {}
+
+        def rows4(x, b):
+            return x[b].rearrange("(m t) e -> m t e", t=4)
+
+        def load(dst, x, b, t0, n, name):
+            tl = keep.tile([P, n, 1024], BF16, name="%s_%d_%d" % (name, b, t0), align_bytes=64)
+            nc.sync.dma_start(out=tl[:], in_=rows4(x, b)[:, t0 : t0 + n, :])
+            for i in range(n):
+                dst[b, t0 + i] = tl[:, i, :]
+
+        wa_w = keep.tile([P, 2 * D], U8, name="wa_w", align_bytes=64)
+        load(k_in, k, 0, 0, 2, "k")
+        load(k_in, k, 0, 2, 2, "k")
+        load(q_in, q, 0, 0, 1, "q")
+        load(q_in, q, 0, 1, 1, "q")
+        load(q_in, q, 0, 2, 2, "q")
+        load(k_in, k, 1, 0, 2, "k")
+        nc.sync.dma_start(out=wa_w[:].bitcast(I32), in_=wa_words[0].bitcast(I32))
+        load(mb_in, mb, 0, 0, 2, "mb")
+        load(x1_in, x1, 0, 0, 2, "x1")
+        load(x2_in, x2, 0, 0, 2, "x2")
+        load(k_in, k, 1, 2, 2, "k")
+        load(q_in, q, 1, 0, 2, "q")
+        load(q_in, q, 1, 2, 2, "q")
+        load(mb_in, mb, 0, 2, 2, "mb")
+        load(x1_in, x1, 0, 2, 2, "x1")
+        load(x2_in, x2, 0, 2, 2, "x2")
+        load(mb_in, mb, 1, 0, 4, "mb")
+        load(x1_in, x1, 1, 0, 4, "x1")
+        load(x2_in, x2, 1, 0, 4, "x2")
+
+        k_codes, k_scales, q_codes, q_scales, banks, grouped = {}, {}, {}, {}, {}, {}
+        for b in range(B):
+            for gr in range(2):
+                k_codes[b, gr] = keep.tile([P, T], U32, name="kc_%d_%d" % (b, gr), align_bytes=64)
+                k_scales[b, gr] = keep.tile([P, T], U8, name="ks_%d_%d" % (b, gr), align_bytes=64)
+            for t in range(4):
+                q_codes[b, t] = keep.tile([P, 2 * P], U32, name="qc_%d_%d" % (b, t), align_bytes=64)
+                q_scales[b, t] = keep.tile([P, 2 * P], U8, name="qs_%d_%d" % (b, t), align_bytes=64)
+
+        def turn(key, blocks, tag="tr"):
+            banks[key] = psum.tile([P, 4, P], F32, name="bank", tag=tag)
+            for i, words in enumerate(blocks):
+                nc.tensor.transpose(banks[key][:, i, :], words, ident[:])
+
+        def words_of(x, gr, u):
+            return x.bitcast(F32)[:, 256 * gr + u : 256 * (gr + 1) : 2]
+
+        def turn_k(b, h, gr, tag="tr"):
+            turn(("k", b, h, gr), [words_of(k_in[b, 2 * h + a], gr, u) for a in range(2) for u in range(2)], tag)
+
+        def turn_q(b, t, tag="tr"):
+            turn(("q", b, t), [words_of(q_in[b, t], gr, u) for gr in range(2) for u in range(2)], tag)
+
+        def group(key, on_vector):
+            grouped[key] = work.tile([P, 1024], BF16, name="grouped", align_bytes=64, bufs=4)
+            dst = grouped[key][:].bitcast(F32).rearrange("p (a m u) -> p a m u", a=2, u=2)
+            src = banks[key][:].rearrange("p (a u) m -> p a m u", u=2)
+            if on_vector:
+                nc.vector.tensor_copy(out=dst, in_=src)
+            else:
+                nc.scalar.copy(out=dst, in_=src)
+
+        def quantize_k(b, h, gr):
+            cols = slice(256 * h, 256 * h + 256)
+            nc.vector.quantize_mx(
+                out=k_codes[b, gr][:, cols].bitcast(E4M3),
+                scales=k_scales[b, gr][:, cols],
+                in_=grouped["k", b, h, gr][:],
+            )
+
+        def quantize_q(b, t):
+            nc.vector.quantize_mx(
+                out=q_codes[b, t][:].bitcast(E4M3), scales=q_scales[b, t][:], in_=grouped["q", b, t][:]
+            )
+
+        lg, mx, nm, den, inv, ex, cb, c_codes, c_scales = {}, {}, {}, {}, {}, {}, {}, {}, {}
+
+        def logits(b, t):
+            lg[b, t] = psum.tile([P, T], F32, name="lg", tag="lg")
+            nc.tensor.matmul_mx(
+                out=lg[b, t][:],
+                lhsT=q_codes[b, t][:, :P].bitcast(E4M3),
+                lhsT_scale=q_scales[b, t][:, :P],
+                rhs=k_codes[b, 0][:].bitcast(E4M3),
+                rhs_scale=k_scales[b, 0][:],
+                start=True,
+                stop=False,
+            )
+            nc.tensor.matmul_mx(
+                out=lg[b, t][:, P * t : P * (t + 1)],
+                lhsT=mask_codes[0][:].bitcast(E4M3),
+                lhsT_scale=mask_scales[0][:],
+                rhs=mask_codes[1][:].bitcast(E4M3),
+                rhs_scale=mask_scales[1][:],
+                start=False,
+                stop=False,
+            )
+            nc.tensor.matmul_mx(
+                out=lg[b, t][:],
+                lhsT=q_codes[b, t][:, P:].bitcast(E4M3),
+                lhsT_scale=q_scales[b, t][:, P:],
+                rhs=k_codes[b, 1][:].bitcast(E4M3),
+                rhs_scale=k_scales[b, 1][:],
+                start=False,
+                stop=True,
+            )
+
+        def row_max(b, t):
+            mx[b, t] = work.tile([P, 1], F32, name="mx", bufs=4)
+            nc.vector.reduce_max(out=mx[b, t][:], in_=lg[b, t][:], axis=AX.X)
+
+        def exponentials(b, t):
+            nm[b, t] = work.tile([P, 1], F32, name="nm", bufs=4)
+            nc.scalar.mul(nm[b, t][:], mx[b, t][:], -1.0 / 32.0)
+            ex[b, t] = work.tile([P, T], F32, name="ex", bufs=4)
+            den[b, t] = work.tile([P, 1], F32, name="den", bufs=4)
+            nc.scalar.activation(
+                out=ex[b, t][:], in_=lg[b, t][:], func=ACT.Exp, bias=nm[b, t][:], scale=1.0 / 32.0,
+                accum_out=den[b, t][:],
+            )
+
+        def invert(b, t):
+            inv[b, t] = work.tile([P, 1], F32, name="inv", bufs=4)
+            nc.vector.reciprocal(inv[b, t][:], den[b, t][:])
+
+        def normalise(b, t):
+            nc.scalar.activation(out=ex[b, t][:], in_=ex[b, t][:], func=ACT.Copy, scale=inv[b, t][:])
+
+        def turn_a(b, t):
+            turn(("a", b, t), [ex[b, t][:, P * s : P * (s + 1)] for s in range(4)])
+
+        def centre(b, t):
+            cb[b, t] = work.tile([P, P, 4], BF16, name="cb", align_bytes=64)
+            nc.vector.scalar_tensor_tensor(
+                out=cb[b, t][:],
+                in0=banks["a", b, t][:].rearrange("p s m -> p m s"),
+                scalar=-1.0 / 512.0,
+                in1=g512[:].unsqueeze(1).to_broadcast([P, P, 4]),
+                op0=ALU.add,
+                op1=ALU.mult,
+            )
+
+        def quantize_c(b, t):
+            c_codes[b, t] = keep.tile([P, P], U32, name="cc_%d_%d" % (b, t), align_bytes=64)
+            c_scales[b, t] = keep.tile([P, P], U8, name="cs_%d_%d" % (b, t), align_bytes=64)
+            nc.vector.quantize_mx(
+                out=c_codes[b, t][:].bitcast(E4M3),
+                scales=c_scales[b, t][:],
+                in_=cb[b, t][:].rearrange("p m s -> p (m s)"),
+            )
+
+        o_tiles, y_scales = {}, {}
+        for b in range(B):
+            o_tiles[b] = keep.tile([P, 4, D], F32, name="o_%d" % b, align_bytes=64)
+            y_scales[b] = keep.tile([P, D], U8, name="ys_%d" % b, align_bytes=64)
+        nb, vt, dif = {}, {}, {}
+
+        def o_of(b, t, c0, c1):
+            return o_tiles[b][:, t, c0:c1]
+
+
+        def difference_v(b, t, c0):
+            cols = slice(c0, c0 + 512)
+            dif[b, t, c0] = work.tile([P, 512], F32, name="dsv", bufs=2)
+            nc.vector.tensor_tensor(
+                out=dif[b, t, c0][:], in0=x2_in[b, t][:, cols], in1=x1_in[b, t][:, cols], op=ALU.subtract
+            )
+
+        def difference_g(b, t, c0):
+            cols = slice(c0, c0 + 512)
+            dif[b, t, c0] = work.tile([P, 512], F32, name="dsb", bufs=DSB)
+            nc.gpsimd.tensor_tensor(
+                out=dif[b, t, c0][:], in0=x2_in[b, t][:, cols], in1=x1_in[b, t][:, cols], op=ALU.subtract
+            )
+
+        def difference_t(b, t, c0):
+            cols = slice(c0, c0 + 512)
+            dif[b, t, c0] = psum.tile([P, 512], F32, name="dif", tag="dif")
+            nc.tensor.matmul(dif[b, t, c0][:], half[0][:], x2_in[b, t][:, cols], start=True, stop=False)
+            nc.tensor.matmul(dif[b, t, c0][:], half[1][:], x1_in[b, t][:, cols], start=False, stop=True)
+
+        def project(b, t, c0):
+            nb[b, t, c0] = psum.tile([P, 512], F32, name="n", tag="n")
+            nc.tensor.matmul_mx(
+                out=nb[b, t, c0][:],
+                lhsT=c_codes[b, t][:].bitcast(E4M3),
+                lhsT_scale=c_scales[b, t][:],
+                rhs=wa_w[:, 2 * c0 : 2 * c0 + 1024].bitcast(E2M1),
+                rhs_scale=wa_s[:, c0 : c0 + 512],
+                start=True,
+                stop=True,
+            )
+
+        def add_bias(b, t, c0):
+            if c0 == 0:
+                vt[b, t] = work.tile([P, D], F32, name="v", bufs=3)
+            nc.vector.tensor_tensor(
+                out=vt[b, t][:, c0 : c0 + 512], in0=nb[b, t, c0][:], in1=mb_in[b, t][:, c0 : c0 + 512], op=ALU.add
+            )
+
+        def gate(b, t, c0, c1):
+            v = vt[b, t][:, c0:c1]
+            nc.scalar.activation(out=v, in_=v, func=ACT.Tanh, scale=0.5)
+
+        def weigh(b, t, c0):
+            nc.vector.scalar_tensor_tensor(
+                out=o_of(b, t, c0, c0 + 512),
+                in0=vt[b, t][:, c0 : c0 + 512],
+                scalar=1.0,
+                in1=dif[b, t, c0][:],
+                op0=ALU.add,
+                op1=ALU.mult,
+            )
+
+        def add_x1(b, t, c0, c1):
+            o = o_of(b, t, c0, c1)
+            x = x1_in[b, t][:, c0:c1]
+            if True:
+                nc.vector.scalar_tensor_tensor(out=o, in0=o, scalar=0.5, in1=x, op0=ALU.mult, op1=ALU.add)
+
+        ybuf, yw = {}, {}
+
+        def store_out(b, t, c0, c1):
+            nc.sync.dma_start(out=rows4(out_0, b)[:, t, c0:c1], in_=o_tiles[b][:, t, c0:c1])
+
+        def regroup(b, c0, c1, on_vector):
+            y = work.tile([P, 256 * 4], BF16, name="y", align_bytes=64, bufs=4)
+            ybuf[b, c0] = y
+            src = o_tiles[b][:, :, c0:c1].rearrange("p t d -> p d t")
+            dst = y[:, : 4 * (c1 - c0)].rearrange("p (d t) -> p d t", t=4)
+            if on_vector:
+                nc.vector.tensor_copy(out=dst, in_=src)
+            else:
+                nc.scalar.copy(out=dst, in_=src)
+
+        def quantize_y(b, c0, c1):
+            w = c1 - c0
+            yw[b, c0] = work.tile([P, 256], U32, name="yw", align_bytes=64, bufs=6)
+            nc.vector.quantize_mx(
+                out=yw[b, c0][:, :w].bitcast(E4M3), scales=y_scales[b][:, c0:c1], in_=ybuf[b, c0][:, : 4 * w]
+            )
+
+        def store_words(b, c0, c1):
+            nc.sync.dma_start(
+                out=out_1[0].rearrange("p m t -> p (m t)")[:, 4 * (D * b + c0) : 4 * (D * b + c1)].bitcast(I32),
+                in_=yw[b, c0][:, : c1 - c0].bitcast(I32),
+            )
+
+        def store_scales(b):
+            for quad in range(4):
+                nc.sync.dma_start(
+                    out=out_2[0, 4 * quad : 4 * quad + 4, D * b : D * (b + 1)].bitcast(I32),
+                    in_=y_scales[b][32 * quad : 32 * quad + 4, :].bitcast(I32),
+                )
+
+        items = [(b, t) for b in range(B) for t in range(4)]
+        units = [(h, gr) for h in range(2) for gr in range(2)]
+        how = ["tt","tt","tg","tg","gg","gg","gg","gg"]
+
+        def differences(i):
+            for j, c0 in enumerate((0, 512)):
+                kind = how[i][j]
+                (difference_t if kind == "t" else difference_g if kind == "g" else difference_v)(*items[i], c0)
+
+        with tc.manual_schedule():
+            tags = ["tr", "n", "dif"]
+            for i, (h, gr) in enumerate(units):
+                turn_k(0, h, gr, tags[i % 3])
+                group(("k", 0, h, gr), False)
+                if i > 0:
+                    quantize_k(0, *units[i - 1])
+            turn_q(0, 0, "n")
+            group(("q", 0, 0), False)
+            quantize_k(0, *units[3])
+            constants_v()
+            turn_q(0, 1, "dif")
+            quantize_q(0, 0)
+            group(("q", 0, 1), True)
+            turn_q(0, 2)
+            logits(0, 0)
+            quantize_q(0, 1)
+            logits(0, 1)
+            turn_k(1, 0, 0, "n")
+            turn_q(0, 3, "dif")
+            row_max(0, 0)
+            exponentials(0, 0)
+            group(("q", 0, 2), False)
+            turn_k(1, 0, 1, "n")
+            row_max(0, 1)
+            group(("k", 1, 0, 0), True)
+            exponentials(0, 1)
+            quantize_q(0, 2)
+            logits(0, 2)
+            invert(0, 0)
+            normalise(0, 0)
+            group(("k", 1, 0, 1), False)
+            quantize_k(1, 0, 0)
+            turn_a(0, 0)
+            invert(0, 1)
+            normalise(0, 1)
+            group(("q", 0, 3), False)
+            row_max(0, 2)
+            exponentials(0, 2)
+            constants_g()
+            quantize_k(1, 0, 1)
+            centre(0, 0)
+            turn_a(0, 1)
+            quantize_q(0, 3)
+            quantize_c(0, 0)
+            project(0, 0, 0)
+            project(0, 0, 512)
+            logits(0, 3)
+            centre(0, 1)
+            turn_k(1, 1, 0)
+            turn_k(1, 1, 1)
+            invert(0, 2)
+            normalise(0, 2)
+            quantize_c(0, 1)
+            project(0, 1, 0)
+            project(0, 1, 512)
+            differences(0)
+            add_bias(0, 0, 0)
+            add_bias(0, 0, 512)
+            gate(0, 0, 0, D)
+            row_max(0, 3)
+            group(("k", 1, 1, 0), False)
+            group(("k", 1, 1, 1), False)
+            exponentials(0, 3)
+            add_bias(0, 1, 0)
+            add_bias(0, 1, 512)
+            gate(0, 1, 0, D)
+            turn_a(0, 2)
+            turn_q(1, 0)
+            group(("q", 1, 0), False)
+            centre(0, 2)
+            quantize_k(1, 1, 0)
+            quantize_k(1, 1, 1)
+            quantize_c(0, 2)
+            project(0, 2, 0)
+            project(0, 2, 512)
+            weigh(0, 0, 0)
+            weigh(0, 0, 512)
+            differences(1)
+            quantize_q(1, 0)
+            turn_q(1, 1)
+            logits(1, 0)
+            weigh(0, 1, 0)
+            weigh(0, 1, 512)
+            add_x1(0, 0, 0, D)
+            store_out(0, 0, 0, D)
+            for s in range(3, 8):
+                cur = items[s] if s < 8 else None
+                p1 = items[s - 1]
+                p2 = items[s - 2]
+                n1 = items[s + 1] if s + 1 < 8 else None
+                n2 = items[s + 2] if s + 2 < 8 else None
+                n3 = items[s + 3] if s + 3 < 8 else None
+                yc = 256 * (s - 5)
+                if n1:
+                    row_max(*n1)
+                if cur:
+                    invert(*cur)
+                    normalise(*cur)
+                    turn_a(*cur)
+                if n1:
+                    exponentials(*n1)
+                differences(s - 1)
+                add_bias(*p1, 0)
+                add_bias(*p1, 512)
+                if n2:
+                    group(("q",) + n2, False)
+                if n3:
+                    turn_q(*n3)
+                add_x1(*p2, 0, D)
+                store_out(*p2, 0, D)
+                if n2:
+                    quantize_q(*n2)
+                    logits(*n2)
+                gate(*p1, 0, D)
+                if cur:
+                    centre(*cur)
+                if 5 <= s <= 7:
+                    regroup(0, yc, yc + 256, False)
+                weigh(*p1, 0)
+                if cur:
+                    quantize_c(*cur)
+                    project(*cur, 0)
+                    project(*cur, 512)
+                weigh(*p1, 512)
+                if 5 <= s <= 7:
+                    quantize_y(0, yc, yc + 256)
+                    store_words(0, yc, yc + 256)
+            differences(7)
+            add_bias(1, 3, 0)
+            add_bias(1, 3, 512)
+            gate(1, 3, 0, 512)
+            gate(1, 3, 512, D)
+            add_x1(1, 2, 0, D)
+            store_out(1, 2, 0, D)
+            regroup(0, 768, 1024, False)
+            weigh(1, 3, 0)
+            weigh(1, 3, 512)
+            quantize_y(0, 768, 1024)
+            store_words(0, 768, 1024)
+            store_scales(0)
+            add_x1(1, 3, 0, 512)
+            store_out(1, 3, 0, 512)
+            add_x1(1, 3, 512, D)
+            store_out(1, 3, 512, D)
+            for i in range(4):
+                regroup(1, 256 * i, 256 * i + 256, i > 0)
+            for i in range(4):
+                quantize_y(1, 256 * i, 256 * i + 256)
+                store_words(1, 256 * i, 256 * i + 256)
+            store_scales(1)

@@ -67,8 +67,11 @@ def tile_saitsdiagonalmaskedmapblend_x2_kernel(
                 in_=wa_scales[0, 4 * quad : 4 * quad + 4, :].bitcast(I32),
             )
 
+        gneg = keep.tile([P, 4], F32, name="gneg")
+
         def constants_g():
             nc.vector.tensor_scalar_mul(g512[:], g_in[:], 512.0)
+            nc.vector.tensor_scalar_mul(gneg[:], g_in[:], -1.0)
 
         def constants_v():
             for i in range(2):
@@ -218,6 +221,20 @@ def tile_saitsdiagonalmaskedmapblend_x2_kernel(
                 op1=ALU.mult,
             )
 
+        cs = {}
+
+        def centre_s(b, t):
+            cs[b, t] = work.tile([P, 4, P], BF16, name="csep")
+            for i in range(4):
+                nc.scalar.activation(
+                    out=cs[b, t][:, i, :], in_=banks["a", b, t][:, i, :], func=ACT.Identity,
+                    scale=g512[:, i : i + 1], bias=gneg[:, i : i + 1],
+                )
+
+        def interleave_s(b, t):
+            cb[b, t] = work.tile([P, P, 4], BF16, name="cb", align_bytes=64)
+            nc.scalar.copy(out=cb[b, t][:], in_=cs[b, t][:].rearrange("p s m -> p m s"))
+
         def quantize_c(b, t):
             c_codes[b, t] = keep.tile([P, P], U32, name="cc_%d_%d" % (b, t), align_bytes=64)
             c_scales[b, t] = keep.tile([P, P], U8, name="cs_%d_%d" % (b, t), align_bytes=64)
@@ -239,7 +256,7 @@ def tile_saitsdiagonalmaskedmapblend_x2_kernel(
 
         def difference_v(b, t, c0):
             cols = slice(c0, c0 + 512)
-            dif[b, t, c0] = work.tile([P, 512], F32, name="dsv", bufs=2)
+            dif[b, t, c0] = work.tile([P, 512], F32, name="dsv", bufs=4)
             nc.vector.tensor_tensor(
                 out=dif[b, t, c0][:], in0=x2_in[b, t][:, cols], in1=x1_in[b, t][:, cols], op=ALU.subtract
             )
@@ -333,7 +350,7 @@ def tile_saitsdiagonalmaskedmapblend_x2_kernel(
 
         items = [(b, t) for b in range(B) for t in range(4)]
         units = [(h, gr) for h in range(2) for gr in range(2)]
-        how = ["tt","tt","tg","tg","gg","gg","gg","gg"]
+        how = ["vv","vv","tt","tt","tt","vv","vv","vv"]
 
         def differences(i):
             for j, c0 in enumerate((0, 512)):
@@ -396,7 +413,6 @@ def tile_saitsdiagonalmaskedmapblend_x2_kernel(
             quantize_c(0, 1)
             project(0, 1, 0)
             project(0, 1, 512)
-            differences(0)
             add_bias(0, 0, 0)
             add_bias(0, 0, 512)
             gate(0, 0, 0, D)
@@ -404,12 +420,14 @@ def tile_saitsdiagonalmaskedmapblend_x2_kernel(
             group(("k", 1, 1, 0), False)
             group(("k", 1, 1, 1), False)
             exponentials(0, 3)
+            differences(0)
             add_bias(0, 1, 0)
             add_bias(0, 1, 512)
             gate(0, 1, 0, D)
             turn_a(0, 2)
             turn_q(1, 0)
             group(("q", 1, 0), False)
+            differences(1)
             centre(0, 2)
             quantize_k(1, 1, 0)
             quantize_k(1, 1, 1)
@@ -418,56 +436,57 @@ def tile_saitsdiagonalmaskedmapblend_x2_kernel(
             project(0, 2, 512)
             weigh(0, 0, 0)
             weigh(0, 0, 512)
-            differences(1)
             quantize_q(1, 0)
             turn_q(1, 1)
             logits(1, 0)
             weigh(0, 1, 0)
             weigh(0, 1, 512)
+            invert(0, 3)
+            normalise(0, 3)
             add_x1(0, 0, 0, D)
             store_out(0, 0, 0, D)
             for s in range(3, 8):
-                cur = items[s] if s < 8 else None
+                cur = items[s]
                 p1 = items[s - 1]
                 p2 = items[s - 2]
                 n1 = items[s + 1] if s + 1 < 8 else None
                 n2 = items[s + 2] if s + 2 < 8 else None
                 n3 = items[s + 3] if s + 3 < 8 else None
                 yc = 256 * (s - 5)
+                if n2:
+                    group(("q",) + n2, False)
+                turn_a(*cur)
                 if n1:
                     row_max(*n1)
-                if cur:
-                    invert(*cur)
-                    normalise(*cur)
-                    turn_a(*cur)
-                if n1:
-                    exponentials(*n1)
+                centre_s(*cur)
+                interleave_s(*cur)
                 differences(s - 1)
                 add_bias(*p1, 0)
                 add_bias(*p1, 512)
                 if n2:
-                    group(("q",) + n2, False)
-                if n3:
-                    turn_q(*n3)
+                    quantize_q(*n2)
+                gate(*p1, 0, D)
+                if n2:
+                    logits(*n2)
+                if n1:
+                    exponentials(*n1)
                 add_x1(*p2, 0, D)
                 store_out(*p2, 0, D)
-                if n2:
-                    quantize_q(*n2)
-                    logits(*n2)
-                gate(*p1, 0, D)
-                if cur:
-                    centre(*cur)
+                quantize_c(*cur)
+                project(*cur, 0)
+                project(*cur, 512)
+                if 6 <= s <= 7:
+                    quantize_y(0, yc - 256, yc)
+                    store_words(0, yc - 256, yc)
+                weigh(*p1, 0)
+                weigh(*p1, 512)
+                if n1:
+                    invert(*n1)
+                    normalise(*n1)
+                if n3:
+                    turn_q(*n3)
                 if 5 <= s <= 7:
                     regroup(0, yc, yc + 256, False)
-                weigh(*p1, 0)
-                if cur:
-                    quantize_c(*cur)
-                    project(*cur, 0)
-                    project(*cur, 512)
-                weigh(*p1, 512)
-                if 5 <= s <= 7:
-                    quantize_y(0, yc, yc + 256)
-                    store_words(0, yc, yc + 256)
             differences(7)
             add_bias(1, 3, 0)
             add_bias(1, 3, 512)
@@ -476,18 +495,21 @@ def tile_saitsdiagonalmaskedmapblend_x2_kernel(
             add_x1(1, 2, 0, D)
             store_out(1, 2, 0, D)
             regroup(0, 768, 1024, False)
+            quantize_y(0, 512, 768)
+            store_words(0, 512, 768)
             weigh(1, 3, 0)
             weigh(1, 3, 512)
-            quantize_y(0, 768, 1024)
-            store_words(0, 768, 1024)
-            store_scales(0)
             add_x1(1, 3, 0, 512)
             store_out(1, 3, 0, 512)
             add_x1(1, 3, 512, D)
             store_out(1, 3, 512, D)
-            for i in range(4):
-                regroup(1, 256 * i, 256 * i + 256, i > 0)
-            for i in range(4):
+            quantize_y(0, 768, 1024)
+            store_words(0, 768, 1024)
+            store_scales(0)
+            regroup(1, 0, 256, False)
+            for i in range(1, 4):
+                regroup(1, 256 * i, 256 * i + 256, True)
+            for i in (1, 0, 2, 3):
                 quantize_y(1, 256 * i, 256 * i + 256)
                 store_words(1, 256 * i, 256 * i + 256)
             store_scales(1)

@@ -19,7 +19,6 @@ ACT = mybir.ActivationFunctionType
 AX = mybir.AxisListType
 
 MASK = 2.0**20
-DSB = 3
 
 
 def tile_saitsdiagonalmaskedmapblend_x2_kernel(
@@ -31,13 +30,10 @@ def tile_saitsdiagonalmaskedmapblend_x2_kernel(
         work = ctx.enter_context(tc.tile_pool(name="work", bufs=3))
         psum = ctx.enter_context(tc.psum_pool(name="psum", bufs=2))
 
-        wa_s = keep.tile([P, D], U8, name="wa_s", align_bytes=64)
-        nc.vector.memset(wa_s[:].bitcast(I32), 0)
         ident = keep.tile([P, P], F32, name="ident")
         make_identity(nc, ident[:])
-        g_in = keep.tile([P, 4], BF16, name="g_in")
-        g512 = keep.tile([P, 4], F32, name="g512")
-
+        wa_s = keep.tile([P, D], U8, name="wa_s", align_bytes=64)
+        nc.vector.memset(wa_s[:].bitcast(I32), 0)
         mask_codes, mask_scales, diags = [], [], []
         for i, value in enumerate((MASK, -MASK)):
             diag = keep.tile([P, 4 * P], BF16, name="diag%d" % i, align_bytes=64)
@@ -54,137 +50,114 @@ def tile_saitsdiagonalmaskedmapblend_x2_kernel(
             diags.append(diag)
             mask_codes.append(keep.tile([P, P], U32, name="mc%d" % i, align_bytes=64))
             mask_scales.append(keep.tile([P, P], U8, name="ms%d" % i, align_bytes=64))
-        half = []
-        for i, value in enumerate((1.0, -1.0)):
-            hi = keep.tile([P, P], BF16, name="half%d" % i)
-            nc.gpsimd.tensor_scalar(out=hi[:], in0=ident[:], scalar1=value, scalar2=0.0, op0=ALU.mult, op1=ALU.add)
-            half.append(hi)
+        g_in = keep.tile([P, 4], BF16, name="g_in")
+        signed = []
+        for i, value in enumerate((0.5, -0.5)):
+            si = keep.tile([P, P], BF16, name="signed%d" % i)
+            nc.gpsimd.tensor_scalar(out=si[:], in0=ident[:], scalar1=value, scalar2=0.0, op0=ALU.mult, op1=ALU.add)
+            signed.append(si)
+        g512 = keep.tile([P, 4], F32, name="g512")
 
-        nc.scalar.dma_start(out=g_in[:], in_=g.rearrange("(p t) -> p t", t=4))
-        for quad in range(4):
-            nc.scalar.dma_start(
-                out=wa_s[32 * quad : 32 * quad + 4, :].bitcast(I32),
-                in_=wa_scales[0, 4 * quad : 4 * quad + 4, :].bitcast(I32),
-            )
-
-        gneg = keep.tile([P, 4], F32, name="gneg")
-
-        def constants_g():
-            nc.vector.tensor_scalar_mul(g512[:], g_in[:], 512.0)
-            nc.vector.tensor_scalar_mul(gneg[:], g_in[:], -1.0)
-
-        def constants_v():
+        def quantize_masks():
             for i in range(2):
                 nc.vector.quantize_mx(out=mask_codes[i][:].bitcast(E4M3), scales=mask_scales[i][:], in_=diags[i][:])
 
-        k_in, q_in, mb_in, x1_in, x2_in = {}, {}, {}, {}, {}
+        def scale_gain():
+            nc.vector.tensor_scalar_mul(g512[:], g_in[:], 512.0)
+
+        loaded = {}
+        wa_w = keep.tile([P, 2 * D], U8, name="wa_w", align_bytes=64)
 
         def rows4(x, b):
             return x[b].rearrange("(m t) e -> m t e", t=4)
 
-        def load(dst, x, b, t0, n, name):
+        def load(name, b, t0, n):
+            x = {"q": q, "k": k, "mb": mb, "x1": x1, "x2": x2}[name]
             tl = keep.tile([P, n, 1024], BF16, name="%s_%d_%d" % (name, b, t0), align_bytes=64)
             nc.sync.dma_start(out=tl[:], in_=rows4(x, b)[:, t0 : t0 + n, :])
             for i in range(n):
-                dst[b, t0 + i] = tl[:, i, :]
+                loaded[name, b, t0 + i] = tl[:, i, :]
 
-        wa_w = keep.tile([P, 2 * D], U8, name="wa_w", align_bytes=64)
-        load(k_in, k, 0, 0, 2, "k")
-        load(k_in, k, 0, 2, 2, "k")
-        load(q_in, q, 0, 0, 1, "q")
-        load(q_in, q, 0, 1, 1, "q")
-        load(q_in, q, 0, 2, 2, "q")
-        load(k_in, k, 1, 0, 2, "k")
+        load("q", 0, 0, 1)
+        for t in range(4):
+            load("k", 0, t, 1)
+        load("q", 0, 1, 1)
+        load("q", 0, 2, 2)
+        load("k", 1, 0, 2)
+        nc.sync.dma_start(out=g_in[:], in_=g.rearrange("(p t) -> p t", t=4))
+        for quad in range(4):
+            nc.sync.dma_start(
+                out=wa_s[32 * quad : 32 * quad + 4, :].bitcast(I32),
+                in_=wa_scales[0, 4 * quad : 4 * quad + 4, :].bitcast(I32),
+            )
+        load("mb", 0, 0, 2)
         nc.sync.dma_start(out=wa_w[:].bitcast(I32), in_=wa_words[0].bitcast(I32))
-        load(mb_in, mb, 0, 0, 2, "mb")
-        load(x1_in, x1, 0, 0, 2, "x1")
-        load(x2_in, x2, 0, 0, 2, "x2")
-        load(k_in, k, 1, 2, 2, "k")
-        load(q_in, q, 1, 0, 2, "q")
-        load(q_in, q, 1, 2, 2, "q")
-        load(mb_in, mb, 0, 2, 2, "mb")
-        load(x1_in, x1, 0, 2, 2, "x1")
-        load(x2_in, x2, 0, 2, 2, "x2")
-        load(mb_in, mb, 1, 0, 4, "mb")
-        load(x1_in, x1, 1, 0, 4, "x1")
-        load(x2_in, x2, 1, 0, 4, "x2")
+        load("k", 1, 2, 2)
+        load("x1", 0, 0, 2)
+        load("x2", 0, 0, 2)
+        load("q", 1, 0, 2)
+        load("q", 1, 2, 2)
+        load("mb", 0, 2, 2)
+        load("x1", 0, 2, 2)
+        load("x2", 0, 2, 2)
+        load("mb", 1, 0, 4)
+        load("x1", 1, 0, 4)
+        load("x2", 1, 0, 4)
 
-        k_codes, k_scales, q_codes, q_scales, banks, grouped = {}, {}, {}, {}, {}, {}
-        for b in range(B):
+        banks, grouped = {}, {}
+        codes, scales = {}, {}
+
+        def turn(name, b, t, tag="tr"):
+            banks[name, b, t] = psum.tile([P, 4, P], F32, name="bank", tag=tag)
+            words = loaded[name, b, t].bitcast(F32)
             for gr in range(2):
-                k_codes[b, gr] = keep.tile([P, T], U32, name="kc_%d_%d" % (b, gr), align_bytes=64)
-                k_scales[b, gr] = keep.tile([P, T], U8, name="ks_%d_%d" % (b, gr), align_bytes=64)
-            for t in range(4):
-                q_codes[b, t] = keep.tile([P, 2 * P], U32, name="qc_%d_%d" % (b, t), align_bytes=64)
-                q_scales[b, t] = keep.tile([P, 2 * P], U8, name="qs_%d_%d" % (b, t), align_bytes=64)
+                for u in range(2):
+                    nc.tensor.transpose(
+                        banks[name, b, t][:, 2 * gr + u, :], words[:, 256 * gr + u : 256 * (gr + 1) : 2], ident[:]
+                    )
 
-        def turn(key, blocks, tag="tr"):
-            banks[key] = psum.tile([P, 4, P], F32, name="bank", tag=tag)
-            for i, words in enumerate(blocks):
-                nc.tensor.transpose(banks[key][:, i, :], words, ident[:])
-
-        def words_of(x, gr, u):
-            return x.bitcast(F32)[:, 256 * gr + u : 256 * (gr + 1) : 2]
-
-        def turn_k(b, h, gr, tag="tr"):
-            turn(("k", b, h, gr), [words_of(k_in[b, 2 * h + a], gr, u) for a in range(2) for u in range(2)], tag)
-
-        def turn_q(b, t, tag="tr"):
-            turn(("q", b, t), [words_of(q_in[b, t], gr, u) for gr in range(2) for u in range(2)], tag)
-
-        def group(key, on_vector):
-            grouped[key] = work.tile([P, 1024], BF16, name="grouped", align_bytes=64, bufs=4)
-            dst = grouped[key][:].bitcast(F32).rearrange("p (a m u) -> p a m u", a=2, u=2)
-            src = banks[key][:].rearrange("p (a u) m -> p a m u", u=2)
+        def group(name, b, t, on_vector=False):
+            grouped[name, b, t] = work.tile([P, 2, 4 * P], BF16, name="grouped", align_bytes=64, bufs=4)
+            dst = grouped[name, b, t][:].bitcast(F32).rearrange("p a (m u) -> p a m u", u=2)
+            src = banks[name, b, t][:].rearrange("p (a u) m -> p a m u", u=2)
             if on_vector:
                 nc.vector.tensor_copy(out=dst, in_=src)
             else:
                 nc.scalar.copy(out=dst, in_=src)
 
-        def quantize_k(b, h, gr):
-            cols = slice(256 * h, 256 * h + 256)
+        def quantize(name, b, t):
+            codes[name, b, t] = keep.tile([P, 2 * P], U32, name="c_%s_%d_%d" % (name, b, t), align_bytes=64)
+            scales[name, b, t] = keep.tile([P, 2 * P], U8, name="s_%s_%d_%d" % (name, b, t), align_bytes=64)
             nc.vector.quantize_mx(
-                out=k_codes[b, gr][:, cols].bitcast(E4M3),
-                scales=k_scales[b, gr][:, cols],
-                in_=grouped["k", b, h, gr][:],
-            )
-
-        def quantize_q(b, t):
-            nc.vector.quantize_mx(
-                out=q_codes[b, t][:].bitcast(E4M3), scales=q_scales[b, t][:], in_=grouped["q", b, t][:]
+                out=codes[name, b, t][:].bitcast(E4M3),
+                scales=scales[name, b, t][:],
+                in_=grouped[name, b, t][:].rearrange("p a m -> p (a m)"),
             )
 
         lg, mx, nm, den, inv, ex, cb, c_codes, c_scales = {}, {}, {}, {}, {}, {}, {}, {}, {}
 
-        def logits(b, t):
-            lg[b, t] = psum.tile([P, T], F32, name="lg", tag="lg")
-            nc.tensor.matmul_mx(
-                out=lg[b, t][:],
-                lhsT=q_codes[b, t][:, :P].bitcast(E4M3),
-                lhsT_scale=q_scales[b, t][:, :P],
-                rhs=k_codes[b, 0][:].bitcast(E4M3),
-                rhs_scale=k_scales[b, 0][:],
-                start=True,
-                stop=False,
-            )
-            nc.tensor.matmul_mx(
-                out=lg[b, t][:, P * t : P * (t + 1)],
-                lhsT=mask_codes[0][:].bitcast(E4M3),
-                lhsT_scale=mask_scales[0][:],
-                rhs=mask_codes[1][:].bitcast(E4M3),
-                rhs_scale=mask_scales[1][:],
-                start=False,
-                stop=False,
-            )
-            nc.tensor.matmul_mx(
-                out=lg[b, t][:],
-                lhsT=q_codes[b, t][:, P:].bitcast(E4M3),
-                lhsT_scale=q_scales[b, t][:, P:],
-                rhs=k_codes[b, 1][:].bitcast(E4M3),
-                rhs_scale=k_scales[b, 1][:],
-                start=False,
-                stop=True,
-            )
+        def logits(b, t, slots=range(4)):
+            if (b, t) not in lg:
+                lg[b, t] = psum.tile([P, T], F32, name="lg", tag="lg")
+            for s in slots:
+                out = lg[b, t][:, P * s : P * (s + 1)]
+                passes = [
+                    (codes["q", b, t][:, P * a : P * (a + 1)], scales["q", b, t][:, P * a : P * (a + 1)],
+                     codes["k", b, s][:, P * a : P * (a + 1)], scales["k", b, s][:, P * a : P * (a + 1)])
+                    for a in range(2)
+                ]
+                if s == t:
+                    passes.insert(1, (mask_codes[0][:], mask_scales[0][:], mask_codes[1][:], mask_scales[1][:]))
+                for i, (wc, ws, mc, ms) in enumerate(passes):
+                    nc.tensor.matmul_mx(
+                        out=out,
+                        lhsT=wc.bitcast(E4M3),
+                        lhsT_scale=ws,
+                        rhs=mc.bitcast(E4M3),
+                        rhs_scale=ms,
+                        start=(i == 0),
+                        stop=(i == len(passes) - 1),
+                    )
 
         def row_max(b, t):
             mx[b, t] = work.tile([P, 1], F32, name="mx", bufs=4)
@@ -204,11 +177,16 @@ def tile_saitsdiagonalmaskedmapblend_x2_kernel(
             inv[b, t] = work.tile([P, 1], F32, name="inv", bufs=4)
             nc.vector.reciprocal(inv[b, t][:], den[b, t][:])
 
-        def normalise(b, t):
-            nc.scalar.activation(out=ex[b, t][:], in_=ex[b, t][:], func=ACT.Copy, scale=inv[b, t][:])
+        def normalise(b, t, on_vector=False):
+            if on_vector:
+                nc.vector.tensor_scalar_mul(ex[b, t][:], ex[b, t][:], inv[b, t][:])
+            else:
+                nc.scalar.activation(out=ex[b, t][:], in_=ex[b, t][:], func=ACT.Copy, scale=inv[b, t][:])
 
-        def turn_a(b, t):
-            turn(("a", b, t), [ex[b, t][:, P * s : P * (s + 1)] for s in range(4)])
+        def turn_map(b, t):
+            banks["a", b, t] = psum.tile([P, 4, P], F32, name="bank", tag="tr")
+            for s in range(4):
+                nc.tensor.transpose(banks["a", b, t][:, s, :], ex[b, t][:, P * s : P * (s + 1)], ident[:])
 
         def centre(b, t):
             cb[b, t] = work.tile([P, P, 4], BF16, name="cb", align_bytes=64)
@@ -220,20 +198,6 @@ def tile_saitsdiagonalmaskedmapblend_x2_kernel(
                 op0=ALU.add,
                 op1=ALU.mult,
             )
-
-        cs = {}
-
-        def centre_s(b, t):
-            cs[b, t] = work.tile([P, 4, P], BF16, name="csep")
-            for i in range(4):
-                nc.scalar.activation(
-                    out=cs[b, t][:, i, :], in_=banks["a", b, t][:, i, :], func=ACT.Identity,
-                    scale=g512[:, i : i + 1], bias=gneg[:, i : i + 1],
-                )
-
-        def interleave_s(b, t):
-            cb[b, t] = work.tile([P, P, 4], BF16, name="cb", align_bytes=64)
-            nc.scalar.copy(out=cb[b, t][:], in_=cs[b, t][:].rearrange("p s m -> p m s"))
 
         def quantize_c(b, t):
             c_codes[b, t] = keep.tile([P, P], U32, name="cc_%d_%d" % (b, t), align_bytes=64)
@@ -249,96 +213,95 @@ def tile_saitsdiagonalmaskedmapblend_x2_kernel(
             o_tiles[b] = keep.tile([P, 4, D], F32, name="o_%d" % b, align_bytes=64)
             y_scales[b] = keep.tile([P, D], U8, name="ys_%d" % b, align_bytes=64)
         nb, vt, dif = {}, {}, {}
+        HALVES = (0, 512)
 
-        def o_of(b, t, c0, c1):
-            return o_tiles[b][:, t, c0:c1]
+        def difference_on_gpsimd(b, t):
+            dif[b, t] = work.tile([P, D], F32, name="ds", tag="ds", bufs=1)
+            for c0 in HALVES:
+                cols = slice(c0, c0 + 512)
+                nc.gpsimd.tensor_tensor(
+                    out=dif[b, t][:, cols],
+                    in0=loaded["x2", b, t][:, cols],
+                    in1=loaded["x1", b, t][:, cols],
+                    op=ALU.subtract,
+                )
 
+        def difference_on_vector(b, t):
+            dif[b, t] = work.tile([P, D], F32, name="ds", tag="ds", bufs=1)
+            nc.vector.tensor_tensor(out=dif[b, t][:], in0=loaded["x2", b, t], in1=loaded["x1", b, t], op=ALU.subtract)
 
-        def difference_v(b, t, c0):
-            cols = slice(c0, c0 + 512)
-            dif[b, t, c0] = work.tile([P, 512], F32, name="dsv", bufs=4)
-            nc.vector.tensor_tensor(
-                out=dif[b, t, c0][:], in0=x2_in[b, t][:, cols], in1=x1_in[b, t][:, cols], op=ALU.subtract
-            )
+        def difference_on_tensor(b, t):
+            for c0 in HALVES:
+                cols = slice(c0, c0 + 512)
+                dif[b, t, c0] = psum.tile([P, 512], F32, name="dif", tag="dif")
+                nc.tensor.matmul(dif[b, t, c0][:], signed[0][:], loaded["x2", b, t][:, cols], start=True, stop=False)
+                nc.tensor.matmul(dif[b, t, c0][:], signed[1][:], loaded["x1", b, t][:, cols], start=False, stop=True)
 
-        def difference_g(b, t, c0):
-            cols = slice(c0, c0 + 512)
-            dif[b, t, c0] = work.tile([P, 512], F32, name="dsb", bufs=DSB)
-            nc.gpsimd.tensor_tensor(
-                out=dif[b, t, c0][:], in0=x2_in[b, t][:, cols], in1=x1_in[b, t][:, cols], op=ALU.subtract
-            )
+        def project(b, t):
+            for c0 in HALVES:
+                nb[b, t, c0] = psum.tile([P, 512], F32, name="n", tag="n")
+                nc.tensor.matmul_mx(
+                    out=nb[b, t, c0][:],
+                    lhsT=c_codes[b, t][:].bitcast(E4M3),
+                    lhsT_scale=c_scales[b, t][:],
+                    rhs=wa_w[:, 2 * c0 : 2 * c0 + 1024].bitcast(E2M1),
+                    rhs_scale=wa_s[:, c0 : c0 + 512],
+                    start=True,
+                    stop=True,
+                )
 
-        def difference_t(b, t, c0):
-            cols = slice(c0, c0 + 512)
-            dif[b, t, c0] = psum.tile([P, 512], F32, name="dif", tag="dif")
-            nc.tensor.matmul(dif[b, t, c0][:], half[0][:], x2_in[b, t][:, cols], start=True, stop=False)
-            nc.tensor.matmul(dif[b, t, c0][:], half[1][:], x1_in[b, t][:, cols], start=False, stop=True)
+        def add_bias(b, t):
+            vt[b, t] = work.tile([P, D], F32, name="v", bufs=3)
+            for c0 in HALVES:
+                cols = slice(c0, c0 + 512)
+                nc.vector.tensor_tensor(
+                    out=vt[b, t][:, cols], in0=nb[b, t, c0][:], in1=loaded["mb", b, t][:, cols], op=ALU.add
+                )
 
-        def project(b, t, c0):
-            nb[b, t, c0] = psum.tile([P, 512], F32, name="n", tag="n")
-            nc.tensor.matmul_mx(
-                out=nb[b, t, c0][:],
-                lhsT=c_codes[b, t][:].bitcast(E4M3),
-                lhsT_scale=c_scales[b, t][:],
-                rhs=wa_w[:, 2 * c0 : 2 * c0 + 1024].bitcast(E2M1),
-                rhs_scale=wa_s[:, c0 : c0 + 512],
-                start=True,
-                stop=True,
-            )
-
-        def add_bias(b, t, c0):
-            if c0 == 0:
-                vt[b, t] = work.tile([P, D], F32, name="v", bufs=3)
-            nc.vector.tensor_tensor(
-                out=vt[b, t][:, c0 : c0 + 512], in0=nb[b, t, c0][:], in1=mb_in[b, t][:, c0 : c0 + 512], op=ALU.add
-            )
-
-        def gate(b, t, c0, c1):
+        def gate(b, t, c0=0, c1=D):
             v = vt[b, t][:, c0:c1]
             nc.scalar.activation(out=v, in_=v, func=ACT.Tanh, scale=0.5)
 
-        def weigh(b, t, c0):
-            nc.vector.scalar_tensor_tensor(
-                out=o_of(b, t, c0, c0 + 512),
-                in0=vt[b, t][:, c0 : c0 + 512],
-                scalar=1.0,
-                in1=dif[b, t, c0][:],
-                op0=ALU.add,
-                op1=ALU.mult,
-            )
+        def weigh(b, t, c0=0, c1=D):
+            if (b, t) in dif:
+                pieces = [(c0, c1, dif[b, t][:, c0:c1])]
+            else:
+                pieces = [(c, c + 512, dif[b, t, c][:]) for c in HALVES]
+            for a, e, d in pieces:
+                nc.vector.scalar_tensor_tensor(
+                    out=o_tiles[b][:, t, a:e], in0=vt[b, t][:, a:e], scalar=1.0, in1=d, op0=ALU.add, op1=ALU.mult
+                )
 
-        def add_x1(b, t, c0, c1):
-            o = o_of(b, t, c0, c1)
-            x = x1_in[b, t][:, c0:c1]
-            if True:
+        def add_x1(b, t, c0=0, c1=D, on_gpsimd=False):
+            o = o_tiles[b][:, t, c0:c1]
+            x = loaded["x1", b, t][:, c0:c1]
+            if (b, t) in dif:
                 nc.vector.scalar_tensor_tensor(out=o, in0=o, scalar=0.5, in1=x, op0=ALU.mult, op1=ALU.add)
+            else:
+                (nc.gpsimd if on_gpsimd else nc.vector).tensor_tensor(out=o, in0=o, in1=x, op=ALU.add)
+            nc.sync.dma_start(out=rows4(out_0, b)[:, t, c0:c1], in_=o)
 
         ybuf, yw = {}, {}
 
-        def store_out(b, t, c0, c1):
-            nc.sync.dma_start(out=rows4(out_0, b)[:, t, c0:c1], in_=o_tiles[b][:, t, c0:c1])
-
-        def regroup(b, c0, c1, on_vector):
-            y = work.tile([P, 256 * 4], BF16, name="y", align_bytes=64, bufs=4)
-            ybuf[b, c0] = y
-            src = o_tiles[b][:, :, c0:c1].rearrange("p t d -> p d t")
-            dst = y[:, : 4 * (c1 - c0)].rearrange("p (d t) -> p d t", t=4)
+        def regroup(b, c0, on_vector=False):
+            ybuf[b, c0] = work.tile([P, 256, 4], BF16, name="y", align_bytes=64, bufs=4)
+            src = o_tiles[b][:, :, c0 : c0 + 256].rearrange("p t (c i) -> p c t i", i=4)
+            dst = ybuf[b, c0][:].rearrange("p (c i) t -> p c t i", i=4)
             if on_vector:
                 nc.vector.tensor_copy(out=dst, in_=src)
             else:
                 nc.scalar.copy(out=dst, in_=src)
 
-        def quantize_y(b, c0, c1):
-            w = c1 - c0
+        def quantize_y(b, c0):
             yw[b, c0] = work.tile([P, 256], U32, name="yw", align_bytes=64, bufs=6)
             nc.vector.quantize_mx(
-                out=yw[b, c0][:, :w].bitcast(E4M3), scales=y_scales[b][:, c0:c1], in_=ybuf[b, c0][:, : 4 * w]
+                out=yw[b, c0][:].bitcast(E4M3),
+                scales=y_scales[b][:, c0 : c0 + 256],
+                in_=ybuf[b, c0][:].rearrange("p d t -> p (d t)"),
             )
-
-        def store_words(b, c0, c1):
+            m0 = 4 * (D * b + c0)
             nc.sync.dma_start(
-                out=out_1[0].rearrange("p m t -> p (m t)")[:, 4 * (D * b + c0) : 4 * (D * b + c1)].bitcast(I32),
-                in_=yw[b, c0][:, : c1 - c0].bitcast(I32),
+                out=out_1[0].rearrange("p m t -> p (m t)")[:, m0 : m0 + 1024].bitcast(I32), in_=yw[b, c0][:].bitcast(I32)
             )
 
         def store_scales(b):
@@ -349,167 +312,192 @@ def tile_saitsdiagonalmaskedmapblend_x2_kernel(
                 )
 
         items = [(b, t) for b in range(B) for t in range(4)]
-        units = [(h, gr) for h in range(2) for gr in range(2)]
-        how = ["vv","vv","tt","tt","tt","vv","vv","vv"]
+        how = ["t","t","v","g","g","g","g","t"]
 
-        def differences(i):
-            for j, c0 in enumerate((0, 512)):
-                kind = how[i][j]
-                (difference_t if kind == "t" else difference_g if kind == "g" else difference_v)(*items[i], c0)
+        def difference(i):
+            (difference_on_tensor if how[i] == "t" else difference_on_gpsimd if how[i] == "g" else difference_on_vector)(*items[i])
 
         with tc.manual_schedule():
-            tags = ["tr", "n", "dif"]
-            for i, (h, gr) in enumerate(units):
-                turn_k(0, h, gr, tags[i % 3])
-                group(("k", 0, h, gr), False)
-                if i > 0:
-                    quantize_k(0, *units[i - 1])
-            turn_q(0, 0, "n")
-            group(("q", 0, 0), False)
-            quantize_k(0, *units[3])
-            constants_v()
-            turn_q(0, 1, "dif")
-            quantize_q(0, 0)
-            group(("q", 0, 1), True)
-            turn_q(0, 2)
-            logits(0, 0)
-            quantize_q(0, 1)
-            logits(0, 1)
-            turn_k(1, 0, 0, "n")
-            turn_q(0, 3, "dif")
+            turn("q", 0, 0)
+            turn("k", 0, 0, "n")
+            group("k", 0, 0, True)
+            group("q", 0, 0)
+            turn("k", 0, 1)
+            turn("k", 0, 2, "n")
+            quantize("q", 0, 0)
+            quantize("k", 0, 0)
+            turn("k", 0, 3)
+            group("k", 0, 1)
+            quantize_masks()
+            quantize("k", 0, 1)
+            turn("q", 0, 1, "dif")
+            group("k", 0, 2)
+            quantize("k", 0, 2)
+            group("k", 0, 3)
+            logits(0, 0, range(3))
+            quantize("k", 0, 3)
+            group("q", 0, 1)
+            logits(0, 0, range(3, 4))
+            quantize("q", 0, 1)
             row_max(0, 0)
+            turn("q", 0, 2, "dif")
+            group("q", 0, 2, True)
+            logits(0, 1)
             exponentials(0, 0)
-            group(("q", 0, 2), False)
-            turn_k(1, 0, 1, "n")
-            row_max(0, 1)
-            group(("k", 1, 0, 0), True)
-            exponentials(0, 1)
-            quantize_q(0, 2)
-            logits(0, 2)
+            scale_gain()
+            quantize("q", 0, 2)
+            turn("k", 1, 1, "n")
+            turn("q", 0, 3, "dif")
             invert(0, 0)
-            normalise(0, 0)
-            group(("k", 1, 0, 1), False)
-            quantize_k(1, 0, 0)
-            turn_a(0, 0)
+            normalise(0, 0, True)
+            row_max(0, 1)
+            turn_map(0, 0)
+            turn("k", 1, 0)
+            exponentials(0, 1)
+            group("q", 0, 3, True)
+            group("k", 1, 1)
+            centre(0, 0)
+            logits(0, 2)
+            quantize_c(0, 0)
             invert(0, 1)
+            project(0, 0)
+            group("k", 1, 0)
+            quantize("q", 0, 3)
             normalise(0, 1)
-            group(("q", 0, 3), False)
             row_max(0, 2)
             exponentials(0, 2)
-            constants_g()
-            quantize_k(1, 0, 1)
-            centre(0, 0)
-            turn_a(0, 1)
-            quantize_q(0, 3)
-            quantize_c(0, 0)
-            project(0, 0, 0)
-            project(0, 0, 512)
-            logits(0, 3)
+            add_bias(0, 0)
+            quantize("k", 1, 1)
+            turn("k", 1, 2, "dif")
+            turn_map(0, 1)
             centre(0, 1)
-            turn_k(1, 1, 0)
-            turn_k(1, 1, 1)
-            invert(0, 2)
-            normalise(0, 2)
+            group("k", 1, 2)
+            turn("k", 1, 3, "n")
+            quantize("k", 1, 2)
             quantize_c(0, 1)
-            project(0, 1, 0)
-            project(0, 1, 512)
-            add_bias(0, 0, 0)
-            add_bias(0, 0, 512)
-            gate(0, 0, 0, D)
+            invert(0, 2)
+            logits(0, 3)
+            quantize("k", 1, 0)
+            group("k", 1, 3)
             row_max(0, 3)
-            group(("k", 1, 1, 0), False)
-            group(("k", 1, 1, 1), False)
+            project(0, 1)
+            gate(0, 0)
+            add_bias(0, 1)
+            difference(0)
+            normalise(0, 2)
+            quantize("k", 1, 3)
+            turn_map(0, 2)
+            weigh(0, 0)
+            turn("q", 1, 0, "n")
             exponentials(0, 3)
-            differences(0)
-            add_bias(0, 1, 0)
-            add_bias(0, 1, 512)
-            gate(0, 1, 0, D)
-            turn_a(0, 2)
-            turn_q(1, 0)
-            group(("q", 1, 0), False)
-            differences(1)
-            centre(0, 2)
-            quantize_k(1, 1, 0)
-            quantize_k(1, 1, 1)
-            quantize_c(0, 2)
-            project(0, 2, 0)
-            project(0, 2, 512)
-            weigh(0, 0, 0)
-            weigh(0, 0, 512)
-            quantize_q(1, 0)
-            turn_q(1, 1)
-            logits(1, 0)
-            weigh(0, 1, 0)
-            weigh(0, 1, 512)
             invert(0, 3)
+            gate(0, 1)
+            turn("q", 1, 1)
             normalise(0, 3)
-            add_x1(0, 0, 0, D)
-            store_out(0, 0, 0, D)
-            for s in range(3, 8):
-                cur = items[s]
-                p1 = items[s - 1]
-                p2 = items[s - 2]
-                n1 = items[s + 1] if s + 1 < 8 else None
-                n2 = items[s + 2] if s + 2 < 8 else None
-                n3 = items[s + 3] if s + 3 < 8 else None
-                yc = 256 * (s - 5)
-                if n2:
-                    group(("q",) + n2, False)
-                turn_a(*cur)
-                if n1:
-                    row_max(*n1)
-                centre_s(*cur)
-                interleave_s(*cur)
-                differences(s - 1)
-                add_bias(*p1, 0)
-                add_bias(*p1, 512)
-                if n2:
-                    quantize_q(*n2)
-                gate(*p1, 0, D)
-                if n2:
-                    logits(*n2)
-                if n1:
-                    exponentials(*n1)
-                add_x1(*p2, 0, D)
-                store_out(*p2, 0, D)
-                quantize_c(*cur)
-                project(*cur, 0)
-                project(*cur, 512)
-                if 6 <= s <= 7:
-                    quantize_y(0, yc - 256, yc)
-                    store_words(0, yc - 256, yc)
-                weigh(*p1, 0)
-                weigh(*p1, 512)
-                if n1:
-                    invert(*n1)
-                    normalise(*n1)
-                if n3:
-                    turn_q(*n3)
-                if 5 <= s <= 7:
-                    regroup(0, yc, yc + 256, False)
-            differences(7)
-            add_bias(1, 3, 0)
-            add_bias(1, 3, 512)
+            difference(1)
+            centre(0, 2)
+            difference(2)
+            group("q", 1, 0)
+            difference(3)
+            add_x1(0, 0)
+            difference(4)
+            turn_map(0, 3)
+            quantize("q", 1, 0)
+            turn("q", 1, 2, "n")
+            logits(1, 0)
+            quantize_c(0, 2)
+            group("q", 1, 2)
+            centre(0, 3)
+            project(0, 2)
+            weigh(0, 1)
+            group("q", 1, 1)
+            row_max(1, 0)
+            quantize_c(0, 3)
+            add_bias(0, 2)
+            exponentials(1, 0)
+            turn("q", 1, 3, "dif")
+            quantize("q", 1, 1)
+            project(0, 3)
+            gate(0, 2)
+            invert(1, 0)
+            add_x1(0, 1)
+            weigh(0, 2)
+            normalise(1, 0)
+            logits(1, 1)
+            quantize("q", 1, 2)
+            group("q", 1, 3)
+            add_bias(0, 3)
+            row_max(1, 1)
+            gate(0, 3)
+            turn_map(1, 0)
+            centre(1, 0)
+            exponentials(1, 1)
+            add_x1(0, 2)
+            quantize_c(1, 0)
+            logits(1, 2)
+            weigh(0, 3)
+            quantize("q", 1, 3)
+            invert(1, 1)
+            project(1, 0)
+            normalise(1, 1)
+            turn_map(1, 1)
+            row_max(1, 2)
+            difference(5)
+            exponentials(1, 2)
+            add_bias(1, 0)
+            centre(1, 1)
+            difference(6)
+            invert(1, 2)
+            add_x1(0, 3)
+            gate(1, 0)
+            normalise(1, 2)
+            weigh(1, 0)
+            logits(1, 3)
+            quantize_c(1, 1)
+            turn_map(1, 2)
+            regroup(0, 0)
+            project(1, 1)
+            row_max(1, 3)
+            centre(1, 2)
+            add_bias(1, 1)
+            exponentials(1, 3)
+            invert(1, 3)
+            gate(1, 1)
+            normalise(1, 3)
+            difference(7)
+            add_x1(1, 0)
+            quantize_c(1, 2)
+            project(1, 2)
+            regroup(0, 512)
+            turn_map(1, 3)
+            weigh(1, 1)
+            quantize_y(0, 0)
+            centre(1, 3)
+            add_bias(1, 2)
+            quantize_c(1, 3)
+            regroup(0, 256)
+            gate(1, 2)
+            add_x1(1, 1)
+            weigh(1, 2)
+            project(1, 3)
+            add_bias(1, 3)
             gate(1, 3, 0, 512)
             gate(1, 3, 512, D)
-            add_x1(1, 2, 0, D)
-            store_out(1, 2, 0, D)
-            regroup(0, 768, 1024, False)
-            quantize_y(0, 512, 768)
-            store_words(0, 512, 768)
-            weigh(1, 3, 0)
-            weigh(1, 3, 512)
+            quantize_y(0, 512)
+            add_x1(1, 2)
+            regroup(0, 768)
+            weigh(1, 3)
             add_x1(1, 3, 0, 512)
-            store_out(1, 3, 0, 512)
+            regroup(1, 0)
             add_x1(1, 3, 512, D)
-            store_out(1, 3, 512, D)
-            quantize_y(0, 768, 1024)
-            store_words(0, 768, 1024)
+            quantize_y(0, 768)
+            regroup(1, 256)
+            quantize_y(0, 256)
             store_scales(0)
-            regroup(1, 0, 256, False)
-            for i in range(1, 4):
-                regroup(1, 256 * i, 256 * i + 256, True)
-            for i in (1, 0, 2, 3):
-                quantize_y(1, 256 * i, 256 * i + 256)
-                store_words(1, 256 * i, 256 * i + 256)
+            regroup(1, 768, True)
+            regroup(1, 512, True)
+            quantize_y(1, 0)
+            quantize_y(1, 768)
+            quantize_y(1, 256)
+            quantize_y(1, 512)
             store_scales(1)

@@ -34,22 +34,20 @@ def tile_saitsdiagonalmaskedmapblend_x2_kernel(
         make_identity(nc, ident[:])
         wa_s = keep.tile([P, D], U8, name="wa_s", align_bytes=64)
         nc.vector.memset(wa_s[:].bitcast(I32), 0)
-        mask_codes, mask_scales, diags = [], [], []
+        diag = keep.tile([P, 2, 4 * P], BF16, name="diag", align_bytes=64)
+        nc.gpsimd.memset(diag[:], 0.0)
         for i, value in enumerate((MASK, -MASK)):
-            diag = keep.tile([P, 4 * P], BF16, name="diag%d" % i, align_bytes=64)
-            nc.gpsimd.memset(diag[:], 0.0)
             nc.gpsimd.affine_select(
-                out=diag[:],
-                in_=diag[:],
+                out=diag[:, i, :],
+                in_=diag[:, i, :],
                 compare_op=ALU.not_equal,
                 fill=value,
                 base=0,
                 pattern=[[-1, 4 * P]],
                 channel_multiplier=4,
             )
-            diags.append(diag)
-            mask_codes.append(keep.tile([P, P], U32, name="mc%d" % i, align_bytes=64))
-            mask_scales.append(keep.tile([P, P], U8, name="ms%d" % i, align_bytes=64))
+        mask_codes = keep.tile([P, 2 * P], U32, name="mask_codes", align_bytes=64)
+        mask_scales = keep.tile([P, 2 * P], U8, name="mask_scales", align_bytes=64)
         g_in = keep.tile([P, 4], BF16, name="g_in")
         signed = []
         for i, value in enumerate((0.5, -0.5)):
@@ -57,15 +55,18 @@ def tile_saitsdiagonalmaskedmapblend_x2_kernel(
             nc.gpsimd.tensor_scalar(out=si[:], in0=ident[:], scalar1=value, scalar2=0.0, op0=ALU.mult, op1=ALU.add)
             signed.append(si)
         g512 = keep.tile([P, 4], F32, name="g512")
+        gneg = keep.tile([P, 4], F32, name="gneg")
 
         def quantize_masks():
-            for i in range(2):
-                nc.vector.quantize_mx(out=mask_codes[i][:].bitcast(E4M3), scales=mask_scales[i][:], in_=diags[i][:])
+            nc.vector.quantize_mx(
+                out=mask_codes[:].bitcast(E4M3), scales=mask_scales[:], in_=diag[:].rearrange("p i m -> p (i m)")
+            )
 
         def scale_gain():
             nc.vector.tensor_scalar_mul(g512[:], g_in[:], 512.0)
+            nc.vector.tensor_scalar_mul(gneg[:], g_in[:], -1.0)
 
-        loaded = {}
+        loaded, pairs = {}, {}
         wa_w = keep.tile([P, 2 * D], U8, name="wa_w", align_bytes=64)
 
         def rows4(x, b):
@@ -77,6 +78,8 @@ def tile_saitsdiagonalmaskedmapblend_x2_kernel(
             nc.sync.dma_start(out=tl[:], in_=rows4(x, b)[:, t0 : t0 + n, :])
             for i in range(n):
                 loaded[name, b, t0 + i] = tl[:, i, :]
+                if i % 2 == 0 and n > 1:
+                    pairs[name, b, t0 + i] = tl[:, i : i + 2, :]
 
         load("q", 0, 0, 1)
         for t in range(4):
@@ -106,6 +109,17 @@ def tile_saitsdiagonalmaskedmapblend_x2_kernel(
 
         banks, grouped = {}, {}
         codes, scales = {}, {}
+        UNITS = {
+            ("q", 0): [(0, 1), (1, 1), (2, 2)],
+            ("k", 0): [(0, 1), (1, 1), (2, 1), (3, 1)],
+            ("k", 1): [(0, 2), (2, 2)],
+            ("q", 1): [(0, 2), (2, 2)],
+        }
+        unit_of = {}
+        for (name, b), units in UNITS.items():
+            for t0, n in units:
+                for i in range(n):
+                    unit_of[name, b, t0 + i] = (t0, n)
 
         def turn(name, b, t, tag="tr"):
             banks[name, b, t] = psum.tile([P, 4, P], F32, name="bank", tag=tag)
@@ -117,22 +131,29 @@ def tile_saitsdiagonalmaskedmapblend_x2_kernel(
                     )
 
         def group(name, b, t, on_vector=False):
-            grouped[name, b, t] = work.tile([P, 2, 4 * P], BF16, name="grouped", align_bytes=64, bufs=4)
-            dst = grouped[name, b, t][:].bitcast(F32).rearrange("p a (m u) -> p a m u", u=2)
+            t0, n = unit_of[name, b, t]
+            if (name, b, t0) not in grouped:
+                grouped[name, b, t0] = work.tile([P, n, 2, 4 * P], BF16, name="grouped%d" % n, align_bytes=64, bufs=4)
+            dst = grouped[name, b, t0][:, t - t0].bitcast(F32).rearrange("p a (m u) -> p a m u", u=2)
             src = banks[name, b, t][:].rearrange("p (a u) m -> p a m u", u=2)
             if on_vector:
                 nc.vector.tensor_copy(out=dst, in_=src)
             else:
                 nc.scalar.copy(out=dst, in_=src)
 
-        def quantize(name, b, t):
-            codes[name, b, t] = keep.tile([P, 2 * P], U32, name="c_%s_%d_%d" % (name, b, t), align_bytes=64)
-            scales[name, b, t] = keep.tile([P, 2 * P], U8, name="s_%s_%d_%d" % (name, b, t), align_bytes=64)
+        def quantize(name, b, t0):
+            n = unit_of[name, b, t0][1]
+            words = keep.tile([P, n * 2 * P], U32, name="c_%s_%d_%d" % (name, b, t0), align_bytes=64)
+            bytes8 = keep.tile([P, n * 2 * P], U8, name="s_%s_%d_%d" % (name, b, t0), align_bytes=64)
             nc.vector.quantize_mx(
-                out=codes[name, b, t][:].bitcast(E4M3),
-                scales=scales[name, b, t][:],
-                in_=grouped[name, b, t][:].rearrange("p a m -> p (a m)"),
+                out=words[:].bitcast(E4M3),
+                scales=bytes8[:],
+                in_=grouped[name, b, t0][:].rearrange("p n a m -> p (n a m)"),
             )
+            for i in range(n):
+                cols = slice(2 * P * i, 2 * P * (i + 1))
+                codes[name, b, t0 + i] = words[:, cols]
+                scales[name, b, t0 + i] = bytes8[:, cols]
 
         lg, mx, nm, den, inv, ex, cb, c_codes, c_scales = {}, {}, {}, {}, {}, {}, {}, {}, {}
 
@@ -147,7 +168,7 @@ def tile_saitsdiagonalmaskedmapblend_x2_kernel(
                     for a in range(2)
                 ]
                 if s == t:
-                    passes.insert(1, (mask_codes[0][:], mask_scales[0][:], mask_codes[1][:], mask_scales[1][:]))
+                    passes.insert(1, (mask_codes[:, :P], mask_scales[:, :P], mask_codes[:, P:], mask_scales[:, P:]))
                 for i, (wc, ws, mc, ms) in enumerate(passes):
                     nc.tensor.matmul_mx(
                         out=out,
@@ -167,46 +188,65 @@ def tile_saitsdiagonalmaskedmapblend_x2_kernel(
             nm[b, t] = work.tile([P, 1], F32, name="nm", bufs=4)
             nc.scalar.mul(nm[b, t][:], mx[b, t][:], -1.0 / 32.0)
             ex[b, t] = work.tile([P, T], F32, name="ex", bufs=4)
-            den[b, t] = work.tile([P, 1], F32, name="den", bufs=4)
             nc.scalar.activation(
                 out=ex[b, t][:], in_=lg[b, t][:], func=ACT.Exp, bias=nm[b, t][:], scale=1.0 / 32.0,
-                accum_out=den[b, t][:],
+                accum_out=den[b][:, t : t + 1],
             )
 
-        def invert(b, t):
-            inv[b, t] = work.tile([P, 1], F32, name="inv", bufs=4)
-            nc.vector.reciprocal(inv[b, t][:], den[b, t][:])
+        for b in range(B):
+            den[b] = keep.tile([P, 4], F32, name="den%d" % b)
+            inv[b] = keep.tile([P, 4], F32, name="inv%d" % b)
+
+        def invert(b, t0, n=1):
+            nc.vector.reciprocal(inv[b][:, t0 : t0 + n], den[b][:, t0 : t0 + n])
 
         def normalise(b, t, on_vector=False):
             if on_vector:
-                nc.vector.tensor_scalar_mul(ex[b, t][:], ex[b, t][:], inv[b, t][:])
+                nc.vector.tensor_scalar_mul(ex[b, t][:], ex[b, t][:], inv[b][:, t : t + 1])
             else:
-                nc.scalar.activation(out=ex[b, t][:], in_=ex[b, t][:], func=ACT.Copy, scale=inv[b, t][:])
+                nc.scalar.activation(out=ex[b, t][:], in_=ex[b, t][:], func=ACT.Copy, scale=inv[b][:, t : t + 1])
 
         def turn_map(b, t):
             banks["a", b, t] = psum.tile([P, 4, P], F32, name="bank", tag="tr")
             for s in range(4):
                 nc.tensor.transpose(banks["a", b, t][:, s, :], ex[b, t][:, P * s : P * (s + 1)], ident[:])
 
-        def centre(b, t):
-            cb[b, t] = work.tile([P, P, 4], BF16, name="cb", align_bytes=64)
+        C_UNIT = {(b, t): (t, 1) for b in range(B) for t in range(4)}
+
+        def centre(b, t, on_scalar=False):
+            t0, n = C_UNIT[b, t]
+            if (b, t0) not in cb:
+                cb[b, t0] = work.tile([P, n, P, 4], BF16, name="cb%d" % n, align_bytes=64, bufs=2)
+            dst = cb[b, t0][:, t - t0]
+            bank = banks["a", b, t]
+            if on_scalar:
+                cs = work.tile([P, 4, P], BF16, name="cs", bufs=2)
+                for i in range(4):
+                    nc.scalar.activation(
+                        out=cs[:, i, :], in_=bank[:, i, :], func=ACT.Identity,
+                        scale=g512[:, i : i + 1], bias=gneg[:, i : i + 1],
+                    )
+                nc.scalar.copy(out=dst, in_=cs[:].rearrange("p s m -> p m s"))
+                return
             nc.vector.scalar_tensor_tensor(
-                out=cb[b, t][:],
-                in0=banks["a", b, t][:].rearrange("p s m -> p m s"),
+                out=dst,
+                in0=bank[:].rearrange("p s m -> p m s"),
                 scalar=-1.0 / 512.0,
                 in1=g512[:].unsqueeze(1).to_broadcast([P, P, 4]),
                 op0=ALU.add,
                 op1=ALU.mult,
             )
 
-        def quantize_c(b, t):
-            c_codes[b, t] = keep.tile([P, P], U32, name="cc_%d_%d" % (b, t), align_bytes=64)
-            c_scales[b, t] = keep.tile([P, P], U8, name="cs_%d_%d" % (b, t), align_bytes=64)
+        def quantize_c(b, t0):
+            n = C_UNIT[b, t0][1]
+            words = keep.tile([P, n * P], U32, name="cc_%d_%d" % (b, t0), align_bytes=64)
+            bytes8 = keep.tile([P, n * P], U8, name="cs_%d_%d" % (b, t0), align_bytes=64)
             nc.vector.quantize_mx(
-                out=c_codes[b, t][:].bitcast(E4M3),
-                scales=c_scales[b, t][:],
-                in_=cb[b, t][:].rearrange("p m s -> p (m s)"),
+                out=words[:].bitcast(E4M3), scales=bytes8[:], in_=cb[b, t0][:].rearrange("p n m s -> p (n m s)")
             )
+            for i in range(n):
+                c_codes[b, t0 + i] = words[:, P * i : P * (i + 1)]
+                c_scales[b, t0 + i] = bytes8[:, P * i : P * (i + 1)]
 
         o_tiles, y_scales = {}, {}
         for b in range(B):
@@ -242,8 +282,8 @@ def tile_saitsdiagonalmaskedmapblend_x2_kernel(
                 nb[b, t, c0] = psum.tile([P, 512], F32, name="n", tag="n")
                 nc.tensor.matmul_mx(
                     out=nb[b, t, c0][:],
-                    lhsT=c_codes[b, t][:].bitcast(E4M3),
-                    lhsT_scale=c_scales[b, t][:],
+                    lhsT=c_codes[b, t].bitcast(E4M3),
+                    lhsT_scale=c_scales[b, t],
                     rhs=wa_w[:, 2 * c0 : 2 * c0 + 1024].bitcast(E2M1),
                     rhs_scale=wa_s[:, c0 : c0 + 512],
                     start=True,
@@ -272,6 +312,15 @@ def tile_saitsdiagonalmaskedmapblend_x2_kernel(
                     out=o_tiles[b][:, t, a:e], in0=vt[b, t][:, a:e], scalar=1.0, in1=d, op0=ALU.add, op1=ALU.mult
                 )
 
+        def add_x1_pair(b, t):
+            o = o_tiles[b][:, t : t + 2, :]
+            x = pairs["x1", b, t]
+            if (b, t) in dif:
+                nc.vector.scalar_tensor_tensor(out=o, in0=o, scalar=0.5, in1=x, op0=ALU.mult, op1=ALU.add)
+            else:
+                nc.vector.tensor_tensor(out=o, in0=o, in1=x, op=ALU.add)
+            nc.sync.dma_start(out=rows4(out_0, b)[:, t : t + 2, :], in_=o)
+
         def add_x1(b, t, c0=0, c1=D, on_gpsimd=False):
             o = o_tiles[b][:, t, c0:c1]
             x = loaded["x1", b, t][:, c0:c1]
@@ -284,24 +333,26 @@ def tile_saitsdiagonalmaskedmapblend_x2_kernel(
         ybuf, yw = {}, {}
 
         def regroup(b, c0, on_vector=False):
-            ybuf[b, c0] = work.tile([P, 256, 4], BF16, name="y", align_bytes=64, bufs=4)
+            h = 512 * (c0 // 512)
+            if (b, h) not in ybuf:
+                ybuf[b, h] = work.tile([P, 512, 4], BF16, name="y", align_bytes=64, bufs=3)
             src = o_tiles[b][:, :, c0 : c0 + 256].rearrange("p t (c i) -> p c t i", i=4)
-            dst = ybuf[b, c0][:].rearrange("p (c i) t -> p c t i", i=4)
+            dst = ybuf[b, h][:, c0 - h : c0 - h + 256, :].rearrange("p (c i) t -> p c t i", i=4)
             if on_vector:
                 nc.vector.tensor_copy(out=dst, in_=src)
             else:
                 nc.scalar.copy(out=dst, in_=src)
 
         def quantize_y(b, c0):
-            yw[b, c0] = work.tile([P, 256], U32, name="yw", align_bytes=64, bufs=6)
+            yw[b, c0] = work.tile([P, 512], U32, name="yw", align_bytes=64, bufs=4)
             nc.vector.quantize_mx(
                 out=yw[b, c0][:].bitcast(E4M3),
-                scales=y_scales[b][:, c0 : c0 + 256],
+                scales=y_scales[b][:, c0 : c0 + 512],
                 in_=ybuf[b, c0][:].rearrange("p d t -> p (d t)"),
             )
             m0 = 4 * (D * b + c0)
             nc.sync.dma_start(
-                out=out_1[0].rearrange("p m t -> p (m t)")[:, m0 : m0 + 1024].bitcast(I32), in_=yw[b, c0][:].bitcast(I32)
+                out=out_1[0].rearrange("p m t -> p (m t)")[:, m0 : m0 + 2048].bitcast(I32), in_=yw[b, c0][:].bitcast(I32)
             )
 
         def store_scales(b):
@@ -312,192 +363,182 @@ def tile_saitsdiagonalmaskedmapblend_x2_kernel(
                 )
 
         items = [(b, t) for b in range(B) for t in range(4)]
-        how = ["t","t","v","g","g","g","g","t"]
 
-        def difference(i):
-            (difference_on_tensor if how[i] == "t" else difference_on_gpsimd if how[i] == "g" else difference_on_vector)(*items[i])
+        def difference(i, how):
+            (difference_on_tensor if how == "t" else difference_on_gpsimd if how == "g" else difference_on_vector)(*items[i])
 
         with tc.manual_schedule():
-            turn("q", 0, 0)
-            turn("k", 0, 0, "n")
-            group("k", 0, 0, True)
-            group("q", 0, 0)
-            turn("k", 0, 1)
-            turn("k", 0, 2, "n")
+            turn("q", 0, 0, "dif")
+            turn("k", 0, 0, "dif")
+            turn("k", 0, 1, "n")
+            group("q", 0, 0, True)
+            turn("k", 0, 2)
             quantize("q", 0, 0)
-            quantize("k", 0, 0)
-            turn("k", 0, 3)
+            turn("k", 0, 3, "dif")
+            turn("q", 0, 1, "dif")
+            group("k", 0, 0)
             group("k", 0, 1)
             quantize_masks()
+            quantize("k", 0, 0)
             quantize("k", 0, 1)
-            turn("q", 0, 1, "dif")
             group("k", 0, 2)
             quantize("k", 0, 2)
             group("k", 0, 3)
-            logits(0, 0, range(3))
-            quantize("k", 0, 3)
             group("q", 0, 1)
-            logits(0, 0, range(3, 4))
+            quantize("k", 0, 3)
             quantize("q", 0, 1)
+            logits(0, 0, range(3))
+            logits(0, 0, range(3, 4))
             row_max(0, 0)
+            turn("q", 0, 3)
             turn("q", 0, 2, "dif")
-            group("q", 0, 2, True)
+            group("q", 0, 3, True)
             logits(0, 1)
+            group("q", 0, 2, True)
             exponentials(0, 0)
-            scale_gain()
-            quantize("q", 0, 2)
-            turn("k", 1, 1, "n")
-            turn("q", 0, 3, "dif")
             invert(0, 0)
             normalise(0, 0, True)
             row_max(0, 1)
+            turn("k", 1, 0, "n")
+            group("k", 1, 0)
+            quantize("q", 0, 2)
+            scale_gain()
+            turn("k", 1, 1, "dif")
             turn_map(0, 0)
-            turn("k", 1, 0)
-            exponentials(0, 1)
-            group("q", 0, 3, True)
-            group("k", 1, 1)
             centre(0, 0)
+            turn("k", 1, 3, "n")
             logits(0, 2)
             quantize_c(0, 0)
-            invert(0, 1)
+            exponentials(0, 1)
             project(0, 0)
-            group("k", 1, 0)
-            quantize("q", 0, 3)
-            normalise(0, 1)
-            row_max(0, 2)
-            exponentials(0, 2)
-            add_bias(0, 0)
-            quantize("k", 1, 1)
-            turn("k", 1, 2, "dif")
-            turn_map(0, 1)
-            centre(0, 1)
-            group("k", 1, 2)
-            turn("k", 1, 3, "n")
-            quantize("k", 1, 2)
-            quantize_c(0, 1)
-            invert(0, 2)
-            logits(0, 3)
-            quantize("k", 1, 0)
+            invert(0, 1)
             group("k", 1, 3)
-            row_max(0, 3)
-            project(0, 1)
+            row_max(0, 2)
+            add_bias(0, 0)
+            normalise(0, 1)
+            turn_map(0, 1)
+            turn("k", 1, 2)
+            group("k", 1, 1)
+            centre(0, 1)
+            exponentials(0, 2)
+            invert(0, 2)
+            group("k", 1, 2)
+            logits(0, 3)
+            quantize_c(0, 1)
             gate(0, 0)
-            add_bias(0, 1)
-            difference(0)
-            normalise(0, 2)
-            quantize("k", 1, 3)
-            turn_map(0, 2)
-            weigh(0, 0)
-            turn("q", 1, 0, "n")
+            quantize("k", 1, 0)
+            project(0, 1)
+            row_max(0, 3)
             exponentials(0, 3)
+            difference(0, "t")
+            normalise(0, 2)
+            turn_map(0, 2)
+            add_bias(0, 1)
+            turn("q", 1, 0, "n")
             invert(0, 3)
-            gate(0, 1)
-            turn("q", 1, 1)
-            normalise(0, 3)
-            difference(1)
+            weigh(0, 0)
             centre(0, 2)
-            difference(2)
+            turn("q", 1, 1, "n")
+            turn("q", 1, 3)
+            gate(0, 1)
+            normalise(0, 3)
             group("q", 1, 0)
-            difference(3)
-            add_x1(0, 0)
-            difference(4)
-            turn_map(0, 3)
-            quantize("q", 1, 0)
-            turn("q", 1, 2, "n")
-            logits(1, 0)
-            quantize_c(0, 2)
-            group("q", 1, 2)
-            centre(0, 3)
-            project(0, 2)
-            weigh(0, 1)
             group("q", 1, 1)
-            row_max(1, 0)
-            quantize_c(0, 3)
-            add_bias(0, 2)
-            exponentials(1, 0)
-            turn("q", 1, 3, "dif")
-            quantize("q", 1, 1)
-            project(0, 3)
-            gate(0, 2)
-            invert(1, 0)
-            add_x1(0, 1)
-            weigh(0, 2)
-            normalise(1, 0)
-            logits(1, 1)
-            quantize("q", 1, 2)
+            turn_map(0, 3)
+            turn("q", 1, 2, "dif")
             group("q", 1, 3)
-            add_bias(0, 3)
+            quantize("k", 1, 2)
+            quantize_c(0, 2)
+            difference(2, "v")
+            quantize("q", 1, 0)
+            centre(0, 3, True)
+            project(0, 2)
+            add_bias(0, 2)
+            add_x1(0, 0)
+            quantize_c(0, 3)
+            group("q", 1, 2)
+            gate(0, 2)
+            logits(1, 1)
+            difference(3, "g")
             row_max(1, 1)
-            gate(0, 3)
-            turn_map(1, 0)
-            centre(1, 0)
+            logits(1, 0)
+            row_max(1, 0)
+            difference(1, "t")
             exponentials(1, 1)
-            add_x1(0, 2)
-            quantize_c(1, 0)
-            logits(1, 2)
-            weigh(0, 3)
-            quantize("q", 1, 3)
+            difference(4, "g")
+            weigh(0, 2)
+            quantize("q", 1, 2)
             invert(1, 1)
-            project(1, 0)
+            exponentials(1, 0)
             normalise(1, 1)
-            turn_map(1, 1)
-            row_max(1, 2)
-            difference(5)
-            exponentials(1, 2)
-            add_bias(1, 0)
-            centre(1, 1)
-            difference(6)
-            invert(1, 2)
-            add_x1(0, 3)
-            gate(1, 0)
-            normalise(1, 2)
-            weigh(1, 0)
+            invert(1, 0)
+            project(0, 3)
+            add_bias(0, 3)
+            weigh(0, 1)
+            normalise(1, 0)
+            difference(5, "g")
+            add_x1(0, 2)
+            gate(0, 3)
+            logits(1, 2)
+            turn_map(1, 0)
             logits(1, 3)
-            quantize_c(1, 1)
-            turn_map(1, 2)
-            regroup(0, 0)
-            project(1, 1)
+            turn_map(1, 1)
+            centre(1, 0, True)
+            weigh(0, 3)
+            centre(1, 1, True)
+            quantize_c(1, 0)
+            row_max(1, 2)
             row_max(1, 3)
-            centre(1, 2)
-            add_bias(1, 1)
+            exponentials(1, 2)
+            project(1, 0)
+            add_bias(1, 0)
+            gate(1, 0)
+            invert(1, 2)
+            normalise(1, 2)
+            quantize_c(1, 1)
+            add_x1(0, 1)
+            turn_map(1, 2)
+            weigh(1, 0)
+            project(1, 1)
+            add_x1(0, 3)
             exponentials(1, 3)
             invert(1, 3)
-            gate(1, 1)
             normalise(1, 3)
-            difference(7)
+            centre(1, 2)
+            add_bias(1, 1)
+            gate(1, 1)
+            turn_map(1, 3)
+            centre(1, 3)
             add_x1(1, 0)
             quantize_c(1, 2)
+            difference(7, "t")
             project(1, 2)
-            regroup(0, 512)
-            turn_map(1, 3)
             weigh(1, 1)
-            quantize_y(0, 0)
-            centre(1, 3)
-            add_bias(1, 2)
+            regroup(0, 768)
             quantize_c(1, 3)
-            regroup(0, 256)
-            gate(1, 2)
-            add_x1(1, 1)
-            weigh(1, 2)
+            regroup(0, 512)
+            difference(6, "g")
+            add_bias(1, 2)
+            quantize_y(0, 512)
             project(1, 3)
             add_bias(1, 3)
+            add_x1(1, 1)
+            gate(1, 2)
             gate(1, 3, 0, 512)
+            weigh(1, 2)
             gate(1, 3, 512, D)
-            quantize_y(0, 512)
-            add_x1(1, 2)
-            regroup(0, 768)
+            regroup(0, 256)
+            regroup(0, 0)
             weigh(1, 3)
             add_x1(1, 3, 0, 512)
-            regroup(1, 0)
+            add_x1(1, 2)
             add_x1(1, 3, 512, D)
-            quantize_y(0, 768)
-            regroup(1, 256)
-            quantize_y(0, 256)
-            store_scales(0)
+            quantize_y(0, 0)
+            regroup(1, 0)
             regroup(1, 768, True)
+            regroup(1, 256)
+            store_scales(0)
             regroup(1, 512, True)
-            quantize_y(1, 0)
-            quantize_y(1, 768)
-            quantize_y(1, 256)
             quantize_y(1, 512)
+            quantize_y(1, 0)
             store_scales(1)

from contextlib import ExitStack

import concourse.mybir as mybir
from concourse.masks import make_identity

B, T, E, D = 2, 512, 1024, 1024
P = 128
FLOPS = 2 * B * T * T * E + 2 * B * T * T * D

F32 = mybir.dt.float32
BF16 = mybir.dt.bfloat16
U32 = mybir.dt.uint32
I32 = mybir.dt.int32
U8 = mybir.dt.uint8
E4M3 = mybir.dt.float8_e4m3fn_x4
E2M1 = mybir.dt.float4_e2m1fn_x4
ALU = mybir.AluOpType
ACT = mybir.ActivationFunctionType
AX = mybir.AxisListType

MASK = 2.0**20


def tile_saitsdiagonalmaskedmapblend_x2_kernel(
    tc, q, k, g, wa_words, wa_scales, mb, x1, x2, out_0, out_1, out_2
):
    nc = tc.nc
    with ExitStack() as ctx:
        keep = ctx.enter_context(tc.tile_pool(name="keep", bufs=1))
        work = ctx.enter_context(tc.tile_pool(name="work", bufs=3))
        psum = ctx.enter_context(tc.psum_pool(name="psum", bufs=2))

        ident = keep.tile([P, P], F32, name="ident")
        make_identity(nc, ident[:])
        wa_s = keep.tile([P, D], U8, name="wa_s", align_bytes=64)
        nc.vector.memset(wa_s[:].bitcast(I32), 0)
        diag = keep.tile([P, 2, 4 * P], BF16, name="diag", align_bytes=64)
        nc.gpsimd.memset(diag[:], 0.0)
        for i, value in enumerate((MASK, -MASK)):
            nc.gpsimd.affine_select(
                out=diag[:, i, :],
                in_=diag[:, i, :],
                compare_op=ALU.not_equal,
                fill=value,
                base=0,
                pattern=[[-1, 4 * P]],
                channel_multiplier=4,
            )
        mask_codes = keep.tile([P, 2 * P], U32, name="mask_codes", align_bytes=64)
        mask_scales = keep.tile([P, 2 * P], U8, name="mask_scales", align_bytes=64)
        g_in = keep.tile([P, 4], BF16, name="g_in")
        signed = []
        for i, value in enumerate((0.5, -0.5)):
            si = keep.tile([P, P], BF16, name="signed%d" % i)
            nc.gpsimd.tensor_scalar(out=si[:], in0=ident[:], scalar1=value, scalar2=0.0, op0=ALU.mult, op1=ALU.add)
            signed.append(si)
        g512 = keep.tile([P, 4], F32, name="g512")
        gneg = keep.tile([P, 4], F32, name="gneg")

        def quantize_masks():
            nc.vector.quantize_mx(
                out=mask_codes[:].bitcast(E4M3), scales=mask_scales[:], in_=diag[:].rearrange("p i m -> p (i m)")
            )

        def scale_gain():
            nc.vector.tensor_scalar_mul(g512[:], g_in[:], 512.0)
            nc.vector.tensor_scalar_mul(gneg[:], g_in[:], -1.0)

        loaded, pairs = {}, {}
        wa_w = keep.tile([P, 2 * D], U8, name="wa_w", align_bytes=64)

        def rows4(x, b):
            return x[b].rearrange("(m t) e -> m t e", t=4)

        def load(name, b, t0, n):
            x = {"q": q, "k": k, "mb": mb, "x1": x1, "x2": x2}[name]
            tl = keep.tile([P, n, 1024], BF16, name="%s_%d_%d" % (name, b, t0), align_bytes=64)
            nc.sync.dma_start(out=tl[:], in_=rows4(x, b)[:, t0 : t0 + n, :])
            for i in range(n):
                loaded[name, b, t0 + i] = tl[:, i, :]
                if i % 2 == 0 and n > 1:
                    pairs[name, b, t0 + i] = tl[:, i : i + 2, :]

        load("q", 0, 0, 1)
        for t in range(4):
            load("k", 0, t, 1)
        load("q", 0, 1, 1)
        load("q", 0, 2, 2)
        load("k", 1, 0, 2)
        nc.sync.dma_start(out=g_in[:], in_=g.rearrange("(p t) -> p t", t=4))
        for quad in range(4):
            nc.sync.dma_start(
                out=wa_s[32 * quad : 32 * quad + 4, :].bitcast(I32),
                in_=wa_scales[0, 4 * quad : 4 * quad + 4, :].bitcast(I32),
            )
        load("mb", 0, 0, 2)
        nc.sync.dma_start(out=wa_w[:].bitcast(I32), in_=wa_words[0].bitcast(I32))
        load("k", 1, 2, 2)
        load("x1", 0, 0, 2)
        load("x2", 0, 0, 2)
        load("q", 1, 0, 2)
        load("q", 1, 2, 2)
        load("mb", 0, 2, 2)
        load("x1", 0, 2, 2)
        load("x2", 0, 2, 2)
        load("mb", 1, 0, 4)
        load("x1", 1, 0, 4)
        load("x2", 1, 0, 4)

        banks, grouped = {}, {}
        codes, scales = {}, {}
        UNITS = {
            ("q", 0): [(0, 1), (1, 1), (2, 2)],
            ("k", 0): [(0, 1), (1, 1), (2, 1), (3, 1)],
            ("k", 1): [(0, 2), (2, 2)],
            ("q", 1): [(0, 2), (2, 2)],
        }
        unit_of = {}
        for (name, b), units in UNITS.items():
            for t0, n in units:
                for i in range(n):
                    unit_of[name, b, t0 + i] = (t0, n)

        def turn(name, b, t, tag="tr"):
            banks[name, b, t] = psum.tile([P, 4, P], F32, name="bank", tag=tag)
            words = loaded[name, b, t].bitcast(F32)
            for gr in range(2):
                for u in range(2):
                    nc.tensor.transpose(
                        banks[name, b, t][:, 2 * gr + u, :], words[:, 256 * gr + u : 256 * (gr + 1) : 2], ident[:]
                    )

        def group(name, b, t, on_vector=False):
            t0, n = unit_of[name, b, t]
            if (name, b, t0) not in grouped:
                grouped[name, b, t0] = work.tile([P, n, 2, 4 * P], BF16, name="grouped%d" % n, align_bytes=64, bufs=4)
            dst = grouped[name, b, t0][:, t - t0].bitcast(F32).rearrange("p a (m u) -> p a m u", u=2)
            src = banks[name, b, t][:].rearrange("p (a u) m -> p a m u", u=2)
            if on_vector:
                nc.vector.tensor_copy(out=dst, in_=src)
            else:
                nc.scalar.copy(out=dst, in_=src)

        def quantize(name, b, t0):
            n = unit_of[name, b, t0][1]
            words = keep.tile([P, n * 2 * P], U32, name="c_%s_%d_%d" % (name, b, t0), align_bytes=64)
            bytes8 = keep.tile([P, n * 2 * P], U8, name="s_%s_%d_%d" % (name, b, t0), align_bytes=64)
            nc.vector.quantize_mx(
                out=words[:].bitcast(E4M3),
                scales=bytes8[:],
                in_=grouped[name, b, t0][:].rearrange("p n a m -> p (n a m)"),
            )
            for i in range(n):
                cols = slice(2 * P * i, 2 * P * (i + 1))
                codes[name, b, t0 + i] = words[:, cols]
                scales[name, b, t0 + i] = bytes8[:, cols]

        lg, mx, nm, den, inv, ex, cb, c_codes, c_scales = {}, {}, {}, {}, {}, {}, {}, {}, {}

        def logits(b, t, slots=range(4)):
            if (b, t) not in lg:
                lg[b, t] = psum.tile([P, T], F32, name="lg", tag="lg")
            for s in slots:
                out = lg[b, t][:, P * s : P * (s + 1)]
                passes = [
                    (codes["q", b, t][:, P * a : P * (a + 1)], scales["q", b, t][:, P * a : P * (a + 1)],
                     codes["k", b, s][:, P * a : P * (a + 1)], scales["k", b, s][:, P * a : P * (a + 1)])
                    for a in range(2)
                ]
                if s == t:
                    passes.insert(1, (mask_codes[:, :P], mask_scales[:, :P], mask_codes[:, P:], mask_scales[:, P:]))
                for i, (wc, ws, mc, ms) in enumerate(passes):
                    nc.tensor.matmul_mx(
                        out=out,
                        lhsT=wc.bitcast(E4M3),
                        lhsT_scale=ws,
                        rhs=mc.bitcast(E4M3),
                        rhs_scale=ms,
                        start=(i == 0),
                        stop=(i == len(passes) - 1),
                    )

        def row_max(b, t):
            mx[b, t] = work.tile([P, 1], F32, name="mx", bufs=4)
            nc.vector.reduce_max(out=mx[b, t][:], in_=lg[b, t][:], axis=AX.X)

        def exponentials(b, t):
            nm[b, t] = work.tile([P, 1], F32, name="nm", bufs=4)
            nc.scalar.mul(nm[b, t][:], mx[b, t][:], -1.0 / 32.0)
            ex[b, t] = work.tile([P, T], F32, name="ex", bufs=4)
            nc.scalar.activation(
                out=ex[b, t][:], in_=lg[b, t][:], func=ACT.Exp, bias=nm[b, t][:], scale=1.0 / 32.0,
                accum_out=den[b][:, t : t + 1],
            )

        for b in range(B):
            den[b] = keep.tile([P, 4], F32, name="den%d" % b)
            inv[b] = keep.tile([P, 4], F32, name="inv%d" % b)

        def invert(b, t0, n=1):
            nc.vector.reciprocal(inv[b][:, t0 : t0 + n], den[b][:, t0 : t0 + n])

        def normalise(b, t, on_vector=False):
            if on_vector:
                nc.vector.tensor_scalar_mul(ex[b, t][:], ex[b, t][:], inv[b][:, t : t + 1])
            else:
                nc.scalar.activation(out=ex[b, t][:], in_=ex[b, t][:], func=ACT.Copy, scale=inv[b][:, t : t + 1])

        def turn_map(b, t):
            banks["a", b, t] = psum.tile([P, 4, P], F32, name="bank", tag="tr")
            for s in range(4):
                nc.tensor.transpose(banks["a", b, t][:, s, :], ex[b, t][:, P * s : P * (s + 1)], ident[:])

        C_UNIT = {(b, t): (t, 1) for b in range(B) for t in range(4)}

        def centre(b, t, on_scalar=False):
            t0, n = C_UNIT[b, t]
            if (b, t0) not in cb:
                cb[b, t0] = work.tile([P, n, P, 4], BF16, name="cb%d" % n, align_bytes=64, bufs=2)
            dst = cb[b, t0][:, t - t0]
            bank = banks["a", b, t]
            if on_scalar:
                cs = work.tile([P, 4, P], BF16, name="cs", bufs=2)
                for i in range(4):
                    nc.scalar.activation(
                        out=cs[:, i, :], in_=bank[:, i, :], func=ACT.Identity,
                        scale=g512[:, i : i + 1], bias=gneg[:, i : i + 1],
                    )
                nc.scalar.copy(out=dst, in_=cs[:].rearrange("p s m -> p m s"))
                return
            nc.vector.scalar_tensor_tensor(
                out=dst,
                in0=bank[:].rearrange("p s m -> p m s"),
                scalar=-1.0 / 512.0,
                in1=g512[:].unsqueeze(1).to_broadcast([P, P, 4]),
                op0=ALU.add,
                op1=ALU.mult,
            )

        def quantize_c(b, t0):
            n = C_UNIT[b, t0][1]
            words = keep.tile([P, n * P], U32, name="cc_%d_%d" % (b, t0), align_bytes=64)
            bytes8 = keep.tile([P, n * P], U8, name="cs_%d_%d" % (b, t0), align_bytes=64)
            nc.vector.quantize_mx(
                out=words[:].bitcast(E4M3), scales=bytes8[:], in_=cb[b, t0][:].rearrange("p n m s -> p (n m s)")
            )
            for i in range(n):
                c_codes[b, t0 + i] = words[:, P * i : P * (i + 1)]
                c_scales[b, t0 + i] = bytes8[:, P * i : P * (i + 1)]

        o_tiles, y_scales = {}, {}
        for b in range(B):
            o_tiles[b] = keep.tile([P, 4, D], F32, name="o_%d" % b, align_bytes=64)
            y_scales[b] = keep.tile([P, D], U8, name="ys_%d" % b, align_bytes=64)
        nb, vt, dif = {}, {}, {}
        HALVES = (0, 512)

        def difference_on_gpsimd(b, t):
            dif[b, t] = work.tile([P, D], F32, name="ds", tag="ds", bufs=1)
            for c0 in HALVES:
                cols = slice(c0, c0 + 512)
                nc.gpsimd.tensor_tensor(
                    out=dif[b, t][:, cols],
                    in0=loaded["x2", b, t][:, cols],
                    in1=loaded["x1", b, t][:, cols],
                    op=ALU.subtract,
                )

        def difference_on_vector(b, t):
            dif[b, t] = work.tile([P, D], F32, name="ds", tag="ds", bufs=1)
            nc.vector.tensor_tensor(out=dif[b, t][:], in0=loaded["x2", b, t], in1=loaded["x1", b, t], op=ALU.subtract)

        def difference_on_tensor(b, t):
            for c0 in HALVES:
                cols = slice(c0, c0 + 512)
                dif[b, t, c0] = psum.tile([P, 512], F32, name="dif", tag="dif")
                nc.tensor.matmul(dif[b, t, c0][:], signed[0][:], loaded["x2", b, t][:, cols], start=True, stop=False)
                nc.tensor.matmul(dif[b, t, c0][:], signed[1][:], loaded["x1", b, t][:, cols], start=False, stop=True)

        def project(b, t):
            for c0 in HALVES:
                nb[b, t, c0] = psum.tile([P, 512], F32, name="n", tag="n")
                nc.tensor.matmul_mx(
                    out=nb[b, t, c0][:],
                    lhsT=c_codes[b, t].bitcast(E4M3),
                    lhsT_scale=c_scales[b, t],
                    rhs=wa_w[:, 2 * c0 : 2 * c0 + 1024].bitcast(E2M1),
                    rhs_scale=wa_s[:, c0 : c0 + 512],
                    start=True,
                    stop=True,
                )

        def add_bias(b, t):
            vt[b, t] = work.tile([P, D], F32, name="v", bufs=3)
            for c0 in HALVES:
                cols = slice(c0, c0 + 512)
                nc.vector.tensor_tensor(
                    out=vt[b, t][:, cols], in0=nb[b, t, c0][:], in1=loaded["mb", b, t][:, cols], op=ALU.add
                )

        def gate(b, t, c0=0, c1=D):
            v = vt[b, t][:, c0:c1]
            nc.scalar.activation(out=v, in_=v, func=ACT.Tanh, scale=0.5)

        def weigh(b, t, c0=0, c1=D):
            if (b, t) in dif:
                pieces = [(c0, c1, dif[b, t][:, c0:c1])]
            else:
                pieces = [(c, c + 512, dif[b, t, c][:]) for c in HALVES]
            for a, e, d in pieces:
                nc.vector.scalar_tensor_tensor(
                    out=o_tiles[b][:, t, a:e], in0=vt[b, t][:, a:e], scalar=1.0, in1=d, op0=ALU.add, op1=ALU.mult
                )

        def add_x1_pair(b, t):
            o = o_tiles[b][:, t : t + 2, :]
            x = pairs["x1", b, t]
            if (b, t) in dif:
                nc.vector.scalar_tensor_tensor(out=o, in0=o, scalar=0.5, in1=x, op0=ALU.mult, op1=ALU.add)
            else:
                nc.vector.tensor_tensor(out=o, in0=o, in1=x, op=ALU.add)
            nc.sync.dma_start(out=rows4(out_0, b)[:, t : t + 2, :], in_=o)

        def add_x1(b, t, c0=0, c1=D, on_gpsimd=False):
            o = o_tiles[b][:, t, c0:c1]
            x = loaded["x1", b, t][:, c0:c1]
            if (b, t) in dif:
                nc.vector.scalar_tensor_tensor(out=o, in0=o, scalar=0.5, in1=x, op0=ALU.mult, op1=ALU.add)
            else:
                (nc.gpsimd if on_gpsimd else nc.vector).tensor_tensor(out=o, in0=o, in1=x, op=ALU.add)
            nc.sync.dma_start(out=rows4(out_0, b)[:, t, c0:c1], in_=o)

        ybuf, yw = {}, {}

        def regroup(b, c0, on_vector=False):
            h = 512 * (c0 // 512)
            if (b, h) not in ybuf:
                ybuf[b, h] = work.tile([P, 512, 4], BF16, name="y", align_bytes=64, bufs=3)
            src = o_tiles[b][:, :, c0 : c0 + 256].rearrange("p t (c i) -> p c t i", i=4)
            dst = ybuf[b, h][:, c0 - h : c0 - h + 256, :].rearrange("p (c i) t -> p c t i", i=4)
            if on_vector:
                nc.vector.tensor_copy(out=dst, in_=src)
            else:
                nc.scalar.copy(out=dst, in_=src)

        def quantize_y(b, c0):
            yw[b, c0] = work.tile([P, 512], U32, name="yw", align_bytes=64, bufs=4)
            nc.vector.quantize_mx(
                out=yw[b, c0][:].bitcast(E4M3),
                scales=y_scales[b][:, c0 : c0 + 512],
                in_=ybuf[b, c0][:].rearrange("p d t -> p (d t)"),
            )
            m0 = 4 * (D * b + c0)
            nc.sync.dma_start(
                out=out_1[0].rearrange("p m t -> p (m t)")[:, m0 : m0 + 2048].bitcast(I32), in_=yw[b, c0][:].bitcast(I32)
            )

        def store_scales(b):
            for quad in range(4):
                nc.sync.dma_start(
                    out=out_2[0, 4 * quad : 4 * quad + 4, D * b : D * (b + 1)].bitcast(I32),
                    in_=y_scales[b][32 * quad : 32 * quad + 4, :].bitcast(I32),
                )

        items = [(b, t) for b in range(B) for t in range(4)]

        def difference(i, how):
            (difference_on_tensor if how == "t" else difference_on_gpsimd if how == "g" else difference_on_vector)(*items[i])

        with tc.manual_schedule():
            turn("q", 0, 0, "dif")
            turn("k", 0, 0, "dif")
            turn("k", 0, 1, "n")
            group("q", 0, 0, True)
            turn("k", 0, 2)
            quantize("q", 0, 0)
            turn("k", 0, 3, "dif")
            turn("q", 0, 1, "dif")
            group("k", 0, 0)
            group("k", 0, 1)
            quantize_masks()
            quantize("k", 0, 0)
            quantize("k", 0, 1)
            group("k", 0, 2)
            quantize("k", 0, 2)
            group("k", 0, 3)
            group("q", 0, 1)
            quantize("k", 0, 3)
            quantize("q", 0, 1)
            logits(0, 0, range(3))
            logits(0, 0, range(3, 4))
            row_max(0, 0)
            turn("q", 0, 3)
            turn("q", 0, 2, "dif")
            group("q", 0, 3, True)
            logits(0, 1)
            group("q", 0, 2, True)
            exponentials(0, 0)
            invert(0, 0)
            normalise(0, 0, True)
            row_max(0, 1)
            turn("k", 1, 0, "n")
            group("k", 1, 0)
            quantize("q", 0, 2)
            scale_gain()
            turn("k", 1, 1, "dif")
            turn_map(0, 0)
            centre(0, 0)
            turn("k", 1, 3, "n")
            logits(0, 2)
            quantize_c(0, 0)
            exponentials(0, 1)
            project(0, 0)
            invert(0, 1)
            group("k", 1, 3)
            row_max(0, 2)
            add_bias(0, 0)
            normalise(0, 1)
            turn_map(0, 1)
            turn("k", 1, 2)
            group("k", 1, 1)
            centre(0, 1)
            exponentials(0, 2)
            invert(0, 2)
            group("k", 1, 2)
            logits(0, 3)
            quantize_c(0, 1)
            gate(0, 0)
            quantize("k", 1, 0)
            project(0, 1)
            row_max(0, 3)
            exponentials(0, 3)
            difference(0, "t")
            normalise(0, 2)
            turn_map(0, 2)
            add_bias(0, 1)
            turn("q", 1, 0, "n")
            invert(0, 3)
            weigh(0, 0)
            centre(0, 2)
            turn("q", 1, 1, "n")
            turn("q", 1, 3)
            gate(0, 1)
            normalise(0, 3)
            group("q", 1, 0)
            group("q", 1, 1)
            turn_map(0, 3)
            turn("q", 1, 2, "dif")
            group("q", 1, 3)
            quantize("k", 1, 2)
            quantize_c(0, 2)
            difference(2, "v")
            quantize("q", 1, 0)
            centre(0, 3, True)
            project(0, 2)
            add_bias(0, 2)
            add_x1(0, 0)
            quantize_c(0, 3)
            group("q", 1, 2)
            gate(0, 2)
            logits(1, 1)
            difference(3, "g")
            row_max(1, 1)
            logits(1, 0)
            row_max(1, 0)
            difference(1, "t")
            exponentials(1, 1)
            difference(4, "g")
            weigh(0, 2)
            quantize("q", 1, 2)
            invert(1, 1)
            exponentials(1, 0)
            normalise(1, 1)
            invert(1, 0)
            project(0, 3)
            add_bias(0, 3)
            weigh(0, 1)
            normalise(1, 0)
            difference(5, "g")
            add_x1(0, 2)
            gate(0, 3)
            logits(1, 2)
            turn_map(1, 0)
            logits(1, 3)
            turn_map(1, 1)
            centre(1, 0, True)
            weigh(0, 3)
            centre(1, 1, True)
            quantize_c(1, 0)
            row_max(1, 2)
            row_max(1, 3)
            exponentials(1, 2)
            project(1, 0)
            add_bias(1, 0)
            gate(1, 0)
            invert(1, 2)
            normalise(1, 2)
            quantize_c(1, 1)
            add_x1(0, 1)
            turn_map(1, 2)
            weigh(1, 0)
            project(1, 1)
            add_x1(0, 3)
            exponentials(1, 3)
            invert(1, 3)
            normalise(1, 3)
            centre(1, 2)
            add_bias(1, 1)
            gate(1, 1)
            turn_map(1, 3)
            centre(1, 3)
            add_x1(1, 0)
            quantize_c(1, 2)
            difference(7, "t")
            project(1, 2)
            weigh(1, 1)
            regroup(0, 768)
            quantize_c(1, 3)
            regroup(0, 512)
            difference(6, "g")
            add_bias(1, 2)
            quantize_y(0, 512)
            project(1, 3)
            add_bias(1, 3)
            add_x1(1, 1)
            gate(1, 2)
            gate(1, 3, 0, 512)
            weigh(1, 2)
            gate(1, 3, 512, D)
            regroup(0, 256)
            regroup(0, 0)
            weigh(1, 3)
            add_x1(1, 3, 0, 512)
            add_x1(1, 2)
            add_x1(1, 3, 512, D)
            quantize_y(0, 0)
            regroup(1, 0)
            regroup(1, 768, True)
            regroup(1, 256)
            store_scales(0)
            regroup(1, 512, True)
            quantize_y(1, 512)
            quantize_y(1, 0)
            store_scales(1)
